import numpy as np
import ml_dtypes


def mxq(x, axis, fmt="e4m3"):
    dtype, down = {"e4m3": (ml_dtypes.float8_e4m3fn, 7), "e5m2": (ml_dtypes.float8_e5m2, 14)}[fmt]
    v = np.moveaxis(np.asarray(x, np.float32).astype(ml_dtypes.bfloat16).astype(np.float64), axis, -1)
    blocks = v.reshape(v.shape[:-1] + (-1, 32))
    amax = np.abs(blocks).max(-1, keepdims=True)
    byte = np.maximum(np.where(amax > 0, np.frexp(amax)[1] - 1 + 127, 0) - down, 1)
    scale = np.exp2(byte - 127.0)
    codes = (blocks / scale).astype(np.float32).astype(dtype).astype(np.float64)
    return np.moveaxis((codes * scale).reshape(v.shape), -1, axis)


WIDE = False


def mx_kscale(k):
    if not WIDE:
        return np.ones(k)
    levels = np.array([10, -10, 5, -5, 0])
    if k % 512:
        return np.exp2(np.random.permutation(np.resize(levels, k // 32))).repeat(32)
    a = np.empty((k // 512, 16))
    for p in range(k // 512):
        a[p, :8] = np.random.permutation(np.resize(levels, 8))
        for g in range(8):
            far = levels[np.abs(levels - a[p, g]) >= 10]
            a[p, g + 8] = far[np.random.randint(len(far))]
    return np.exp2(a.ravel()).repeat(32)


def f64(x):
    return np.asarray(x).astype(np.float64)


def striped(idx):
    return np.tile(idx.reshape(-1, 16).T, (8, 1)).astype(np.uint16)


def unstriped(offs):
    return offs[:16].T.reshape(-1).astype(np.int64)


def pack_weight(w):
    k, n = w.shape
    w = f64(np.asarray(w, np.float32).astype(ml_dtypes.bfloat16)).reshape(k // 32, 32, n)
    amax = np.abs(w).max(1)
    byte = np.clip(np.where(amax > 0, np.frexp(amax)[1] - 1 + 127 - 7, 1), 1, 254)
    scaled = (w * np.exp2(127.0 - byte)[:, None, :]).reshape(k, n).astype(np.float32)
    words = np.ascontiguousarray(scaled.reshape(k // 512, 128, 4, n).transpose(0, 1, 3, 2)).astype(ml_dtypes.float8_e4m3fn).view(np.uint8)
    return words, np.ascontiguousarray(byte.astype(np.uint8).reshape(k // 512, 16, n))


def unpack_weight(words, scales):
    g, p, n, _ = words.shape
    vals = np.ascontiguousarray(words).view(ml_dtypes.float8_e4m3fn).astype(np.float64) * np.repeat(np.exp2(scales.astype(np.float64) - 127.0), 8, axis=1)[..., None]
    return vals.transpose(0, 1, 3, 2).reshape(g * 512, n)


K, T, S, H, V, W = 1024, 1024, 512, 512, 512, 2048
P = 2 ** 7


def setup_inputs():
    n = np.random.standard_normal
    s = mx_kscale(K)[:, None]
    u = mx_kscale(H)
    packed_xT = pack_weight(n((K, T)) * s)
    packed_eT = pack_weight(n((H, W)) / np.sqrt(H) / u[:, None])
    return {
        "x_words": packed_xT[0],
        "x_scales": packed_xT[1],
        "w1": (n((K, H)) / np.sqrt(K) / s * u).astype(np.float32),
        "e_words": packed_eT[0],
        "e_scales": packed_eT[1],
        "qn": (np.tile(np.random.uniform(1.5, 2.5, W), (P, 1))).astype(np.float32),
        "own": (np.random.uniform(1.5, 2.5, (S, 1))).astype(np.float32),
        "offs": striped(np.random.permutation(T)[:S]),
        "refs": striped(np.random.permutation(W)[:V]),
    }


def reference(x_words, x_scales, w1, e_words, e_scales, qn, own, offs, refs):
    xq = unpack_weight(x_words, x_scales)[:, unstriped(offs)]
    h = mxq(f64(w1), 0, "e4m3").T @ xq
    e_refs = unpack_weight(e_words, e_scales)[:, unstriped(refs)]
    y = 0.3 * ((mxq(h, 0, "e4m3").T @ e_refs))
    dd = f64(qn)[:1][:, unstriped(refs)] - y + f64(own)
    return y / dd

@@ -1,0 +1,200 @@
+from contextlib import ExitStack
+
+import concourse.mybir as mybir
+from concourse.masks import make_identity
+
+K, T, S, H, V, W = 1024, 1024, 512, 512, 512, 2048
+FLOPS = 2 * K * H * S + 2 * H * S * V
+BYTES = K * T + K * T // 32 + 4 * K * H + H * W + H * W // 32 + 4 * W + 4 * S + 2 * 2 * 128 * 32 + 4 * S * V
+
+F32 = mybir.dt.float32
+BF16 = mybir.dt.bfloat16
+I32 = mybir.dt.int32
+U32 = mybir.dt.uint32
+U16 = mybir.dt.uint16
+U8 = mybir.dt.uint8
+FP8X4 = mybir.dt.float8_e4m3fn_x4
+ALU = mybir.AluOpType
+ACT = mybir.ActivationFunctionType
+
+P = 128
+PACK = 4
+PASSES = K // (P * PACK)
+TILES = S // P
+INV_GAIN = 1.0 / 0.3
+VECTOR_SHARE = (48, 84)
+
+
+def tile_picked_ytani_sim_p_kernel(
+    tc, x_words, x_scales, w1, e_words, e_scales, qn, own, offs, refs, out
+):
+    nc = tc.nc
+    with ExitStack() as ctx:
+        keep = ctx.enter_context(tc.tile_pool(name="keep", bufs=1))
+        psum = ctx.enter_context(tc.psum_pool(name="psum", bufs=1))
+
+        def sbuf(name, shape, dtype, tag=None):
+            return keep.tile(shape, dtype, name=name, tag=tag or name, align_bytes=64)
+
+        def bank(number, shape):
+            return psum.tile(shape, F32, name="bank%d" % number)
+
+        offs_sb = keep.tile([P, S // 16], U16, name="offs_sb")
+        refs_sb = keep.tile([P, V // 16], U16, name="refs_sb")
+        xs_win = sbuf("xs_win", [P, T], U8)
+        es_win = sbuf("es_win", [P, W], U8)
+        qn_win = sbuf("qn_win", [P, W], F32)
+        own_rows = sbuf("own_rows", [P, P], F32)
+        ident = sbuf("ident", [P, P], F32)
+
+        nc.gpsimd.memset(xs_win[:].bitcast(I32), 0)
+        nc.gpsimd.memset(es_win[:].bitcast(I32), 0)
+        nc.vector.memset(own_rows[0 : P - TILES, :], 0.0)
+        nc.vector.memset(qn_win[0 : P - 1, :], 0.0)
+        make_identity(nc, ident[:])
+
+        w_raw = [sbuf("w_raw%d" % o, [P, PACK, H], F32) for o in range(PASSES)]
+        xw_win = [sbuf("xw_win%d" % o, [P, T], I32) for o in range(PASSES)]
+        ew_win = sbuf("ew_win", [P, W], I32)
+
+        def load_w(o):
+            rows = w1[o * P * PACK : (o + 1) * P * PACK, :]
+            nc.sync.dma_start(w_raw[o][:], rows.rearrange("(p j) c -> p j c", j=PACK))
+
+        nc.sync.dma_start(offs_sb[:], offs)
+        nc.sync.dma_start(refs_sb[:], refs)
+        nc.sync.dma_start(qn_win[P - 1 : P, :], qn[0:1, :])
+        for q in range(4):
+            nc.sync.dma_start(
+                xs_win[32 * q : 32 * q + 4 * PASSES, :].bitcast(I32),
+                x_scales[:, 4 * q : 4 * q + 4, :].bitcast(I32),
+            )
+        load_w(0)
+        for q in range(4):
+            nc.sync.dma_start(
+                es_win[32 * q : 32 * q + 4, :].bitcast(I32),
+                e_scales[0, 4 * q : 4 * q + 4, :].bitcast(I32),
+            )
+        load_w(1)
+        for o in range(PASSES):
+            nc.sync.dma_start(
+                xw_win[o][:], x_words[o].rearrange("p n t -> p (n t)").bitcast(I32)
+            )
+        nc.sync.dma_start(ew_win[:], e_words[0].rearrange("p n t -> p (n t)").bitcast(I32))
+        nc.sync.dma_start(own_rows[P - TILES : P, :], own.rearrange("(j p) o -> j (p o)", p=P))
+
+        xs = sbuf("xs", [P, S], U8)
+        nc.vector.tensor_copy(xs[:], xs_win[:].indirect(offs_sb[:]))
+        q_row = sbuf("q_row", [P, V], F32)
+        nc.vector.tensor_scalar(
+            q_row[:], qn_win[:].indirect(refs_sb[:]), INV_GAIN, 0.0, ALU.mult, ALU.add
+        )
+        es = sbuf("es", [P, V], U8)
+        nc.vector.tensor_copy(es[:], es_win[:].indirect(refs_sb[:]))
+
+        turned = bank(4, [P, TILES, P])
+        for b in range(V // P):
+            nc.tensor.transpose(turned[:, b, :], q_row[:, b * P : (b + 1) * P], ident[:])
+        q_cols = sbuf("q_cols", [P, V // P], F32)
+        nc.scalar.copy(q_cols[:], turned[:, :, P - 1])
+        own_turned = bank(5, [P, P])
+        nc.tensor.transpose(own_turned[:], own_rows[:], ident[:])
+        own_cols = sbuf("own_cols", [P, TILES], F32)
+        nc.vector.tensor_scalar(own_cols[:], own_turned[:, P - TILES : P], INV_GAIN, None, ALU.mult)
+        spread = bank(6, [P, V])
+        for b in range(V // P):
+            nc.tensor.transpose(
+                spread[:, b * P : (b + 1) * P], q_cols[:, b : b + 1].to_broadcast([P, P]), ident[:]
+            )
+        q_all = sbuf("q_all", [P, V], F32)
+        nc.scalar.copy(q_all[:], spread[:])
+
+        w_codes, w_scales = [], []
+        for o in range(PASSES):
+            grouped = sbuf("w_grouped%d" % o, [P, PACK * H], BF16)
+            src = w_raw[o][:].rearrange("p j (m t) -> p m j t", t=PACK)
+            dst = grouped[:].rearrange("p (t m j) -> p m j t", t=PACK, j=PACK)
+            cut = P - VECTOR_SHARE[o]
+            nc.scalar.copy(dst[:, 0:cut], src[:, 0:cut])
+            if cut < P:
+                nc.vector.tensor_copy(dst[:, cut:P], src[:, cut:P])
+            codes = sbuf("w_codes%d" % o, [P, H], U32)
+            scales = sbuf("w_scales%d" % o, [P, H], U8)
+            nc.vector.quantize_mx(codes[:].bitcast(FP8X4), scales[:], grouped[:])
+            w_codes.append(codes)
+            w_scales.append(scales)
+
+        xw = [sbuf("xw%d" % o, [P, S], U32) for o in range(PASSES)]
+        for o, lo, hi in ((0, 0, 128), (1, 0, 128), (0, 128, 256), (1, 128, 256), (0, 256, 512), (1, 256, 512)):
+            nc.vector.tensor_copy(
+                xw[o][:, lo:hi],
+                xw_win[o][:].bitcast(U32).indirect(offs_sb[:, lo // 16 : hi // 16]),
+            )
+        ew = sbuf("ew", [P, V], U32)
+        nc.vector.tensor_copy(ew[:], ew_win[:].bitcast(U32).indirect(refs_sb[:]))
+
+        h_codes = sbuf("h_codes", [P, S], U32, tag="ew_win")
+        h_scales = sbuf("h_scales", [P, S], U8)
+
+        def products(j):
+            cols = slice(j * P, (j + 1) * P)
+            h_acc = bank(j, [P, PACK, P])
+            for t in range(PACK):
+                chans = slice(t * P, (t + 1) * P)
+                for o in range(PASSES):
+                    nc.tensor.matmul_mx(
+                        h_acc[:, t, :],
+                        lhsT=w_codes[o][:, chans].bitcast(FP8X4),
+                        lhsT_scale=w_scales[o][:, chans],
+                        rhs=xw[o][:, cols].bitcast(FP8X4),
+                        rhs_scale=xs[4 * o : P, cols],
+                        start=(o == 0),
+                        stop=(o == PASSES - 1),
+                    )
+            grouped = sbuf("h_grouped%d" % j, [P, P, PACK], BF16)
+            nc.scalar.copy(grouped[:], h_acc[:].rearrange("p t n -> p n t"))
+            nc.vector.quantize_mx(
+                h_codes[:, cols].bitcast(FP8X4),
+                h_scales[:, cols],
+                grouped[:].rearrange("p n t -> p (n t)"),
+            )
+            acc = bank(TILES + j, [P, V])
+            nc.tensor.matmul_mx(
+                acc[:],
+                lhsT=h_codes[:, cols].bitcast(FP8X4),
+                lhsT_scale=h_scales[:, cols],
+                rhs=ew[:].bitcast(FP8X4),
+                rhs_scale=es[:],
+                start=True,
+                stop=True,
+            )
+            return acc
+
+        def ratio(j, acc):
+            den = sbuf("den%d" % j, [P, V], F32)
+            nc.vector.scalar_tensor_tensor(
+                den[:], q_all[:], own_cols[:, j : j + 1], acc[:], ALU.add, ALU.subtract
+            )
+            root = sbuf("root%d" % j, [P, V], F32)
+            nc.scalar.activation(root[:], den[:], ACT.Abs_reciprocal_sqrt)
+            inv = sbuf("inv%d" % j, [P, V], F32)
+            nc.scalar.activation(inv[:], root[:], ACT.Square)
+            sign = sbuf("sign%d" % j, [P, V], F32)
+            signed = sbuf("signed%d" % j, [P, V], F32)
+            if j in (2, 3):
+                nc.vector.tensor_scalar(sign[:], den[:], 0.0, 0.5, ALU.is_ge, ALU.subtract)
+                nc.vector.scalar_tensor_tensor(
+                    signed[:], acc[:], 2.0, sign[:], ALU.mult, ALU.mult
+                )
+            else:
+                nc.scalar.activation(sign[:], den[:], ACT.Sign)
+                nc.vector.tensor_tensor(signed[:], acc[:], sign[:], ALU.mult)
+            result = sbuf("result%d" % j, [P, V], F32)
+            nc.vector.tensor_tensor(result[:], signed[:], inv[:], ALU.mult)
+            nc.sync.dma_start(out[j * P : (j + 1) * P, :], result[:])
+
+        accs = [products(0)]
+        for j in range(TILES):
+            if j + 1 < TILES:
+                accs.append(products(j + 1))
+            ratio(j, accs[j])

@@ -95,6 +95,8 @@ def tile_picked_ytani_sim_p_kernel(
         turned = bank(4, [P, TILES, P])
         for b in range(V // P):
             nc.tensor.transpose(turned[:, b, :], q_row[:, b * P : (b + 1) * P], ident[:])
+        warm = sbuf("warm", [P, 1], F32)
+        nc.scalar.activation(warm[:], turned[:, 0, P - 1 : P], ACT.Abs_reciprocal_sqrt)
         q_cols = sbuf("q_cols", [P, V // P], F32)
         nc.scalar.copy(q_cols[:], turned[:, :, P - 1])
         own_turned = bank(5, [P, P])
@@ -123,6 +125,18 @@ def tile_picked_ytani_sim_p_kernel(
             nc.vector.quantize_mx(codes[:].bitcast(FP8X4), scales[:], grouped[:])
             w_codes.append(codes)
             w_scales.append(scales)
+
+        warm_acc = bank(2 * TILES - 1, [P, H])
+        for again in range(3):
+            nc.tensor.matmul_mx(
+                warm_acc[:],
+                lhsT=w_codes[0][:, 0:P].bitcast(FP8X4),
+                lhsT_scale=w_scales[0][:, 0:P],
+                rhs=w_codes[0][:].bitcast(FP8X4),
+                rhs_scale=w_scales[0][:],
+                start=True,
+                stop=True,
+            )
 
         xw = [sbuf("xw%d" % o, [P, S], U32) for o in range(PASSES)]
         for o, lo, hi in ((0, 0, 128), (1, 0, 128), (0, 128, 256), (1, 128, 256), (0, 256, 512), (1, 256, 512)):
@@ -177,8 +191,6 @@ def tile_picked_ytani_sim_p_kernel(
             )
             root = sbuf("root%d" % j, [P, V], F32)
             nc.scalar.activation(root[:], den[:], ACT.Abs_reciprocal_sqrt)
-            inv = sbuf("inv%d" % j, [P, V], F32)
-            nc.scalar.activation(inv[:], root[:], ACT.Square)
             sign = sbuf("sign%d" % j, [P, V], F32)
             signed = sbuf("signed%d" % j, [P, V], F32)
             if j in (2, 3):
@@ -189,9 +201,14 @@ def tile_picked_ytani_sim_p_kernel(
             else:
                 nc.scalar.activation(sign[:], den[:], ACT.Sign)
                 nc.vector.tensor_tensor(signed[:], acc[:], sign[:], ALU.mult)
+            inv = sbuf("inv%d" % j, [P, V], F32)
+            nc.scalar.activation(inv[:], root[:], ACT.Square)
             result = sbuf("result%d" % j, [P, V], F32)
-            nc.vector.tensor_tensor(result[:], signed[:], inv[:], ALU.mult)
-            nc.sync.dma_start(out[j * P : (j + 1) * P, :], result[:])
+            width = V // 2 if j == TILES - 1 else V
+            for lo in range(0, V, width):
+                part = slice(lo, lo + width)
+                nc.vector.tensor_tensor(result[:, part], signed[:, part], inv[:, part], ALU.mult)
+                nc.sync.dma_start(out[j * P : (j + 1) * P, part], result[:, part])
 
         accs = [products(0)]
         for j in range(TILES):

@@ -22,7 +22,8 @@ PACK = 4
 PASSES = K // (P * PACK)
 TILES = S // P
 INV_GAIN = 1.0 / 0.3
-VECTOR_SHARE = (48, 84)
+VECTOR_SHARE = (32, 56)
+X_PIECES = ((0, 128), (128, 256), (256, 512))
 
 
 def tile_picked_ytani_sim_p_kernel(
@@ -31,10 +32,14 @@ def tile_picked_ytani_sim_p_kernel(
     nc = tc.nc
     with ExitStack() as ctx:
         keep = ctx.enter_context(tc.tile_pool(name="keep", bufs=1))
+        shared = ctx.enter_context(tc.tile_pool(name="shared", bufs=1))
         psum = ctx.enter_context(tc.psum_pool(name="psum", bufs=1))
 
         def sbuf(name, shape, dtype, tag=None):
             return keep.tile(shape, dtype, name=name, tag=tag or name, align_bytes=64)
+
+        def placed(name, shape, dtype, offset):
+            return shared.tile(shape, dtype, name=name, offset=offset, align_bytes=64)
 
         def bank(number, shape):
             return psum.tile(shape, F32, name="bank%d" % number)
@@ -44,22 +49,29 @@ def tile_picked_ytani_sim_p_kernel(
         xs_win = sbuf("xs_win", [P, T], U8)
         es_win = sbuf("es_win", [P, W], U8)
         qn_win = sbuf("qn_win", [P, W], F32)
-        own_rows = sbuf("own_rows", [P, P], F32)
+        own_raw = sbuf("own_raw", [P, TILES], F32)
         ident = sbuf("ident", [P, P], F32)
+        warm = sbuf("warm", [P, 2], F32)
 
         nc.gpsimd.memset(xs_win[:].bitcast(I32), 0)
         nc.gpsimd.memset(es_win[:].bitcast(I32), 0)
-        nc.vector.memset(own_rows[0 : P - TILES, :], 0.0)
+        nc.vector.memset(warm[:, 0:1], 1.0)
         nc.vector.memset(qn_win[0 : P - 1, :], 0.0)
         make_identity(nc, ident[:])
+        nc.scalar.activation(warm[:, 1:2], warm[:, 0:1], ACT.Abs_reciprocal_sqrt)
 
-        w_raw = [sbuf("w_raw%d" % o, [P, PACK, H], F32) for o in range(PASSES)]
+        w_raw = [placed("w_raw0", [P, PACK, H], F32, 0), sbuf("w_raw1", [P, PACK, H], F32)]
         xw_win = [sbuf("xw_win%d" % o, [P, T], I32) for o in range(PASSES)]
         ew_win = sbuf("ew_win", [P, W], I32)
 
         def load_w(o):
             rows = w1[o * P * PACK : (o + 1) * P * PACK, :]
             nc.sync.dma_start(w_raw[o][:], rows.rearrange("(p j) c -> p j c", j=PACK))
+
+        def load_x(o):
+            nc.sync.dma_start(
+                xw_win[o][:], x_words[o].rearrange("p n t -> p (n t)").bitcast(I32)
+            )
 
         nc.sync.dma_start(offs_sb[:], offs)
         nc.sync.dma_start(refs_sb[:], refs)
@@ -76,43 +88,32 @@ def tile_picked_ytani_sim_p_kernel(
                 e_scales[0, 4 * q : 4 * q + 4, :].bitcast(I32),
             )
         load_w(1)
-        for o in range(PASSES):
-            nc.sync.dma_start(
-                xw_win[o][:], x_words[o].rearrange("p n t -> p (n t)").bitcast(I32)
-            )
+        load_x(0)
+        load_x(1)
         nc.sync.dma_start(ew_win[:], e_words[0].rearrange("p n t -> p (n t)").bitcast(I32))
-        nc.sync.dma_start(own_rows[P - TILES : P, :], own.rearrange("(j p) o -> j (p o)", p=P))
+        with nc.allow_non_contiguous_dma(reason="one value of own for each partition and tile"):
+            nc.sync.dma_start(own_raw[:], own.rearrange("(j p) o -> p (j o)", p=P))
 
-        xs = sbuf("xs", [P, S], U8)
-        nc.vector.tensor_copy(xs[:], xs_win[:].indirect(offs_sb[:]))
         q_row = sbuf("q_row", [P, V], F32)
         nc.vector.tensor_scalar(
             q_row[:], qn_win[:].indirect(refs_sb[:]), INV_GAIN, 0.0, ALU.mult, ALU.add
         )
+        xs = sbuf("xs", [P, S], U8)
+        nc.vector.tensor_copy(xs[:], xs_win[:].indirect(offs_sb[:]))
         es = sbuf("es", [P, V], U8)
         nc.vector.tensor_copy(es[:], es_win[:].indirect(refs_sb[:]))
 
-        turned = bank(4, [P, TILES, P])
-        for b in range(V // P):
-            nc.tensor.transpose(turned[:, b, :], q_row[:, b * P : (b + 1) * P], ident[:])
-        warm = sbuf("warm", [P, 1], F32)
-        nc.scalar.activation(warm[:], turned[:, 0, P - 1 : P], ACT.Abs_reciprocal_sqrt)
-        q_cols = sbuf("q_cols", [P, V // P], F32)
-        nc.scalar.copy(q_cols[:], turned[:, :, P - 1])
-        own_turned = bank(5, [P, P])
-        nc.tensor.transpose(own_turned[:], own_rows[:], ident[:])
-        own_cols = sbuf("own_cols", [P, TILES], F32)
-        nc.vector.tensor_scalar(own_cols[:], own_turned[:, P - TILES : P], INV_GAIN, None, ALU.mult)
-        spread = bank(6, [P, V])
-        for b in range(V // P):
-            nc.tensor.transpose(
-                spread[:, b * P : (b + 1) * P], q_cols[:, b : b + 1].to_broadcast([P, P]), ident[:]
+        xw = [sbuf("xw%d" % o, [P, S], U32) for o in range(PASSES)]
+
+        def gather_x(o, lo, hi):
+            nc.vector.tensor_copy(
+                xw[o][:, lo:hi],
+                xw_win[o][:].bitcast(U32).indirect(offs_sb[:, lo // 16 : hi // 16]),
             )
-        q_all = sbuf("q_all", [P, V], F32)
-        nc.scalar.copy(q_all[:], spread[:])
 
         w_codes, w_scales = [], []
-        for o in range(PASSES):
+
+        def quantise_w(o):
             grouped = sbuf("w_grouped%d" % o, [P, PACK * H], BF16)
             src = w_raw[o][:].rearrange("p j (m t) -> p m j t", t=PACK)
             dst = grouped[:].rearrange("p (t m j) -> p m j t", t=PACK, j=PACK)
@@ -120,11 +121,13 @@ def tile_picked_ytani_sim_p_kernel(
             nc.scalar.copy(dst[:, 0:cut], src[:, 0:cut])
             if cut < P:
                 nc.vector.tensor_copy(dst[:, cut:P], src[:, cut:P])
-            codes = sbuf("w_codes%d" % o, [P, H], U32)
+            codes = sbuf("w_codes%d" % o, [P, H], U32, tag="es_win" if o == 0 else None)
             scales = sbuf("w_scales%d" % o, [P, H], U8)
             nc.vector.quantize_mx(codes[:].bitcast(FP8X4), scales[:], grouped[:])
             w_codes.append(codes)
             w_scales.append(scales)
+
+        quantise_w(0)
 
         warm_acc = bank(2 * TILES - 1, [P, H])
         for again in range(3):
@@ -138,19 +141,41 @@ def tile_picked_ytani_sim_p_kernel(
                 stop=True,
             )
 
-        xw = [sbuf("xw%d" % o, [P, S], U32) for o in range(PASSES)]
-        for o, lo, hi in ((0, 0, 128), (1, 0, 128), (0, 128, 256), (1, 128, 256), (0, 256, 512), (1, 256, 512)):
-            nc.vector.tensor_copy(
-                xw[o][:, lo:hi],
-                xw_win[o][:].bitcast(U32).indirect(offs_sb[:, lo // 16 : hi // 16]),
+        quantise_w(1)
+        gather_x(0, 0, S)
+        for lo, hi in X_PIECES:
+            gather_x(1, lo, hi)
+
+        turned = bank(4, [P, TILES, P])
+        for b in range(V // P):
+            nc.tensor.transpose(turned[:, b, :], q_row[:, b * P : (b + 1) * P], ident[:])
+        q_cols = sbuf("q_cols", [P, V // P], F32)
+        nc.scalar.copy(q_cols[:], turned[:, :, P - 1])
+        own_first = placed("own_first", [P, 1], F32, 4096 + 128)
+        own_rest = placed("own_rest", [P, TILES - 1], F32, 4096 + 64)
+        nc.gpsimd.tensor_scalar(own_first[:], own_raw[:, 0:1], INV_GAIN, 0.0, ALU.mult, ALU.add)
+        nc.gpsimd.tensor_scalar(own_rest[:], own_raw[:, 1:TILES], INV_GAIN, 0.0, ALU.mult, ALU.add)
+        own_cols = [own_first[:]] + [own_rest[:, j : j + 1] for j in range(TILES - 1)]
+        spread = bank(6, [P, V])
+        for b in range(V // P):
+            nc.tensor.transpose(
+                spread[:, b * P : (b + 1) * P], q_cols[:, b : b + 1].to_broadcast([P, P]), ident[:]
             )
+        q_all = placed("q_all", [P, V], F32, 0)
+        nc.scalar.copy(q_all[:], spread[:])
+
         ew = sbuf("ew", [P, V], U32)
         nc.vector.tensor_copy(ew[:], ew_win[:].bitcast(U32).indirect(refs_sb[:]))
 
-        h_codes = sbuf("h_codes", [P, S], U32, tag="ew_win")
-        h_scales = sbuf("h_scales", [P, S], U8)
+        h_words = sbuf("h_words", [P, S], U32, tag="own_raw")
+        h_codes = [h_words[:, j * P : (j + 1) * P] for j in range(TILES)]
+        h_scales_early = sbuf("h_scales_early", [P, S - P], U8)
+        h_scales_last = placed("h_scales_last", [P, P], U8, 4096 + 128)
+        h_scales = [h_scales_early[:, j * P : (j + 1) * P] for j in range(TILES - 1)]
+        h_scales.append(h_scales_last[:])
+        h_grouped = {}
 
-        def products(j):
+        def hidden(j):
             cols = slice(j * P, (j + 1) * P)
             h_acc = bank(j, [P, PACK, P])
             for t in range(PACK):
@@ -167,16 +192,21 @@ def tile_picked_ytani_sim_p_kernel(
                     )
             grouped = sbuf("h_grouped%d" % j, [P, P, PACK], BF16)
             nc.scalar.copy(grouped[:], h_acc[:].rearrange("p t n -> p n t"))
+            h_grouped[j] = grouped
+
+        def quantise_h(j):
             nc.vector.quantize_mx(
-                h_codes[:, cols].bitcast(FP8X4),
-                h_scales[:, cols],
-                grouped[:].rearrange("p n t -> p (n t)"),
+                h_codes[j].bitcast(FP8X4),
+                h_scales[j],
+                h_grouped[j][:].rearrange("p n t -> p (n t)"),
             )
+
+        def product(j):
             acc = bank(TILES + j, [P, V])
             nc.tensor.matmul_mx(
                 acc[:],
-                lhsT=h_codes[:, cols].bitcast(FP8X4),
-                lhsT_scale=h_scales[:, cols],
+                lhsT=h_codes[j].bitcast(FP8X4),
+                lhsT_scale=h_scales[j],
                 rhs=ew[:].bitcast(FP8X4),
                 rhs_scale=es[:],
                 start=True,
@@ -184,34 +214,78 @@ def tile_picked_ytani_sim_p_kernel(
             )
             return acc
 
-        def ratio(j, acc):
-            den = sbuf("den%d" % j, [P, V], F32)
+        accs, dens, signs, invs, signeds = {}, {}, {}, {}, {}
+
+        def denominator(j):
+            accs[j] = product(j)
+            dens[j] = sbuf("den%d" % j, [P, V], F32)
             nc.vector.scalar_tensor_tensor(
-                den[:], q_all[:], own_cols[:, j : j + 1], acc[:], ALU.add, ALU.subtract
+                dens[j][:], q_all[:], own_cols[j], accs[j][:], ALU.add, ALU.subtract
             )
+
+        def sign_on_scalar(j):
+            signs[j] = sbuf("sign%d" % j, [P, V], F32)
+            nc.scalar.activation(signs[j][:], dens[j][:], ACT.Sign)
+            signeds[j] = 1.0
+
+        def sign_on_vector(j):
+            signs[j] = sbuf("sign%d" % j, [P, V], F32)
+            nc.vector.tensor_scalar(signs[j][:], dens[j][:], 0.0, 0.5, ALU.is_ge, ALU.subtract)
+            signeds[j] = 2.0
+
+        def inverse(j):
             root = sbuf("root%d" % j, [P, V], F32)
-            nc.scalar.activation(root[:], den[:], ACT.Abs_reciprocal_sqrt)
-            sign = sbuf("sign%d" % j, [P, V], F32)
-            signed = sbuf("signed%d" % j, [P, V], F32)
-            if j in (2, 3):
-                nc.vector.tensor_scalar(sign[:], den[:], 0.0, 0.5, ALU.is_ge, ALU.subtract)
-                nc.vector.scalar_tensor_tensor(
-                    signed[:], acc[:], 2.0, sign[:], ALU.mult, ALU.mult
-                )
-            else:
-                nc.scalar.activation(sign[:], den[:], ACT.Sign)
-                nc.vector.tensor_tensor(signed[:], acc[:], sign[:], ALU.mult)
-            inv = sbuf("inv%d" % j, [P, V], F32)
-            nc.scalar.activation(inv[:], root[:], ACT.Square)
+            nc.scalar.activation(root[:], dens[j][:], ACT.Abs_reciprocal_sqrt)
+            invs[j] = sbuf("inv%d" % j, [P, V], F32)
+            nc.scalar.activation(invs[j][:], root[:], ACT.Square)
+
+        def numerator(j):
+            factor = signeds[j]
+            signeds[j] = sbuf("signed%d" % j, [P, V], F32)
+            nc.vector.scalar_tensor_tensor(
+                signeds[j][:], accs[j][:], factor, signs[j][:], ALU.mult, ALU.mult
+            )
+
+        def reciprocal_on_gpsimd(j):
+            invs[j, "signed"] = sbuf("recip%d" % j, [P, V], F32)
+            nc.gpsimd.tensor_tensor(invs[j, "signed"][:], signs[j][:], invs[j][:], ALU.mult)
+
+        def finish_from_bank(j):
             result = sbuf("result%d" % j, [P, V], F32)
-            width = V // 2 if j == TILES - 1 else V
+            nc.vector.scalar_tensor_tensor(
+                result[:], accs[j][:], signeds[j], invs[j, "signed"][:], ALU.mult, ALU.mult
+            )
+            nc.sync.dma_start(out[j * P : (j + 1) * P, :], result[:])
+
+        def finish(j, engine, width):
+            result = sbuf("result%d" % j, [P, V], F32)
             for lo in range(0, V, width):
                 part = slice(lo, lo + width)
-                nc.vector.tensor_tensor(result[:, part], signed[:, part], inv[:, part], ALU.mult)
+                engine.tensor_tensor(result[:, part], signeds[j][:, part], invs[j][:, part], ALU.mult)
                 nc.sync.dma_start(out[j * P : (j + 1) * P, part], result[:, part])
 
-        accs = [products(0)]
         for j in range(TILES):
-            if j + 1 < TILES:
-                accs.append(products(j + 1))
-            ratio(j, accs[j])
+            hidden(j)
+        for j in range(TILES - 1):
+            quantise_h(j)
+        denominator(0)
+        quantise_h(TILES - 1)
+        sign_on_vector(0)
+        inverse(0)
+        denominator(1)
+        sign_on_vector(1)
+        numerator(0)
+        inverse(1)
+        finish(0, nc.gpsimd, V)
+        denominator(2)
+        numerator(1)
+        sign_on_scalar(2)
+        inverse(2)
+        finish(1, nc.gpsimd, V)
+        denominator(3)
+        numerator(2)
+        sign_on_scalar(3)
+        inverse(3)
+        finish(2, nc.gpsimd, V)
+        numerator(3)
+        finish(3, nc.vector, V // 2)

@@ -58,6 +58,8 @@ def tile_picked_ytani_sim_p_kernel(
         nc.vector.memset(warm[:, 0:1], 1.0)
         nc.vector.memset(qn_win[0 : P - 1, :], 0.0)
         make_identity(nc, ident[:])
+        es = sbuf("es", [P, V], U8)
+        nc.gpsimd.memset(es[:].bitcast(I32), 0)
         nc.scalar.activation(warm[:, 1:2], warm[:, 0:1], ACT.Abs_reciprocal_sqrt)
 
         w_raw = [placed("w_raw0", [P, PACK, H], F32, 0), sbuf("w_raw1", [P, PACK, H], F32)]
@@ -82,11 +84,7 @@ def tile_picked_ytani_sim_p_kernel(
                 x_scales[:, 4 * q : 4 * q + 4, :].bitcast(I32),
             )
         load_w(0)
-        for q in range(4):
-            nc.sync.dma_start(
-                es_win[32 * q : 32 * q + 4, :].bitcast(I32),
-                e_scales[0, 4 * q : 4 * q + 4, :].bitcast(I32),
-            )
+        nc.sync.dma_start(es_win[0:P:8, :].bitcast(I32), e_scales[0].bitcast(I32))
         load_w(1)
         load_x(0)
         load_x(1)
@@ -100,8 +98,13 @@ def tile_picked_ytani_sim_p_kernel(
         )
         xs = sbuf("xs", [P, S], U8)
         nc.vector.tensor_copy(xs[:], xs_win[:].indirect(offs_sb[:]))
-        es = sbuf("es", [P, V], U8)
-        nc.vector.tensor_copy(es[:], es_win[:].indirect(refs_sb[:]))
+        es_picked = sbuf("es_picked", [P, V], U8)
+        nc.vector.tensor_copy(es_picked[:], es_win[:].indirect(refs_sb[:]))
+        for q in range(4):
+            nc.sync.dma_start(
+                es[32 * q : 32 * q + 4, :].bitcast(I32),
+                es_picked[32 * q : 32 * q + 32 : 8, :].bitcast(I32),
+            )
 
         xw = [sbuf("xw%d" % o, [P, S], U32) for o in range(PASSES)]
 

@@ -49,7 +49,7 @@ def tile_picked_ytani_sim_p_kernel(
         xs_win = sbuf("xs_win", [P, T], U8)
         es_win = sbuf("es_win", [P, W], U8)
         qn_win = sbuf("qn_win", [P, W], F32)
-        own_raw = sbuf("own_raw", [P, TILES], F32)
+        own_rows = sbuf("own_rows", [P, P], F32)
         ident = sbuf("ident", [P, P], F32)
         warm = sbuf("warm", [P, 2], F32)
 
@@ -57,6 +57,7 @@ def tile_picked_ytani_sim_p_kernel(
         nc.gpsimd.memset(es_win[:].bitcast(I32), 0)
         nc.vector.memset(warm[:, 0:1], 1.0)
         nc.vector.memset(qn_win[0 : P - 1, :], 0.0)
+        nc.gpsimd.memset(own_rows[0 : P - TILES, :], 0.0)
         make_identity(nc, ident[:])
         es = sbuf("es", [P, V], U8)
         nc.gpsimd.memset(es[:].bitcast(I32), 0)
@@ -85,12 +86,11 @@ def tile_picked_ytani_sim_p_kernel(
             )
         load_w(0)
         nc.sync.dma_start(es_win[0:P:8, :].bitcast(I32), e_scales[0].bitcast(I32))
+        nc.sync.dma_start(own_rows[P - TILES : P, :], own.rearrange("(j p) o -> j (p o)", p=P))
         load_w(1)
         load_x(0)
         load_x(1)
         nc.sync.dma_start(ew_win[:], e_words[0].rearrange("p n t -> p (n t)").bitcast(I32))
-        with nc.allow_non_contiguous_dma(reason="one value of own for each partition and tile"):
-            nc.sync.dma_start(own_raw[:], own.rearrange("(j p) o -> p (j o)", p=P))
 
         q_row = sbuf("q_row", [P, V], F32)
         nc.vector.tensor_scalar(
@@ -156,8 +156,11 @@ def tile_picked_ytani_sim_p_kernel(
         nc.scalar.copy(q_cols[:], turned[:, :, P - 1])
         own_first = placed("own_first", [P, 1], F32, 4096 + 128)
         own_rest = placed("own_rest", [P, TILES - 1], F32, 4096 + 64)
-        nc.gpsimd.tensor_scalar(own_first[:], own_raw[:, 0:1], INV_GAIN, 0.0, ALU.mult, ALU.add)
-        nc.gpsimd.tensor_scalar(own_rest[:], own_raw[:, 1:TILES], INV_GAIN, 0.0, ALU.mult, ALU.add)
+        own_turned = bank(5, [P, P])
+        nc.tensor.transpose(own_turned[:], own_rows[:], ident[:])
+        first = P - TILES
+        nc.scalar.activation(own_first[:], own_turned[:, first : first + 1], ACT.Copy, scale=INV_GAIN)
+        nc.scalar.activation(own_rest[:], own_turned[:, first + 1 : P], ACT.Copy, scale=INV_GAIN)
         own_cols = [own_first[:]] + [own_rest[:, j : j + 1] for j in range(TILES - 1)]
         spread = bank(6, [P, V])
         for b in range(V // P):
@@ -170,7 +173,7 @@ def tile_picked_ytani_sim_p_kernel(
         ew = sbuf("ew", [P, V], U32)
         nc.vector.tensor_copy(ew[:], ew_win[:].bitcast(U32).indirect(refs_sb[:]))
 
-        h_words = sbuf("h_words", [P, S], U32, tag="own_raw")
+        h_words = sbuf("h_words", [P, S], U32, tag="es_picked")
         h_codes = [h_words[:, j * P : (j + 1) * P] for j in range(TILES)]
         h_scales_early = sbuf("h_scales_early", [P, S - P], U8)
         h_scales_last = placed("h_scales_last", [P, P], U8, 4096 + 128)

@@ -22,7 +22,8 @@ PACK = 4
 PASSES = K // (P * PACK)
 TILES = S // P
 INV_GAIN = 1.0 / 0.3
-VECTOR_SHARE = (32, 56)
+VECTOR_SHARE = (16, 84)
+TINY = 2.0 ** -120
 X_PIECES = ((0, 128), (128, 256), (256, 512))
 
 
@@ -56,7 +57,7 @@ def tile_picked_ytani_sim_p_kernel(
         nc.gpsimd.memset(xs_win[:].bitcast(I32), 0)
         nc.gpsimd.memset(es_win[:].bitcast(I32), 0)
         nc.vector.memset(warm[:, 0:1], 1.0)
-        nc.vector.memset(qn_win[0 : P - 1, :], 0.0)
+        nc.vector.memset(qn_win[0 : P - 1, :].bitcast(I32), 0)
         nc.gpsimd.memset(own_rows[0 : P - TILES, :], 0.0)
         make_identity(nc, ident[:])
         es = sbuf("es", [P, V], U8)
@@ -76,9 +77,9 @@ def tile_picked_ytani_sim_p_kernel(
                 xw_win[o][:], x_words[o].rearrange("p n t -> p (n t)").bitcast(I32)
             )
 
-        nc.sync.dma_start(offs_sb[:], offs)
         nc.sync.dma_start(refs_sb[:], refs)
         nc.sync.dma_start(qn_win[P - 1 : P, :], qn[0:1, :])
+        nc.sync.dma_start(offs_sb[:], offs)
         for q in range(4):
             nc.sync.dma_start(
                 xs_win[32 * q : 32 * q + 4 * PASSES, :].bitcast(I32),
@@ -86,9 +87,9 @@ def tile_picked_ytani_sim_p_kernel(
             )
         load_w(0)
         nc.sync.dma_start(es_win[0:P:8, :].bitcast(I32), e_scales[0].bitcast(I32))
+        load_x(0)
         nc.sync.dma_start(own_rows[P - TILES : P, :], own.rearrange("(j p) o -> j (p o)", p=P))
         load_w(1)
-        load_x(0)
         load_x(1)
         nc.sync.dma_start(ew_win[:], e_words[0].rearrange("p n t -> p (n t)").bitcast(I32))
 
@@ -124,30 +125,16 @@ def tile_picked_ytani_sim_p_kernel(
             nc.scalar.copy(dst[:, 0:cut], src[:, 0:cut])
             if cut < P:
                 nc.vector.tensor_copy(dst[:, cut:P], src[:, cut:P])
-            codes = sbuf("w_codes%d" % o, [P, H], U32, tag="es_win" if o == 0 else None)
+            codes = sbuf("w_codes%d" % o, [P, H], U32, tag="own_rows" if o == 0 else None)
             scales = sbuf("w_scales%d" % o, [P, H], U8)
             nc.vector.quantize_mx(codes[:].bitcast(FP8X4), scales[:], grouped[:])
             w_codes.append(codes)
             w_scales.append(scales)
 
-        quantise_w(0)
-
-        warm_acc = bank(2 * TILES - 1, [P, H])
-        for again in range(3):
-            nc.tensor.matmul_mx(
-                warm_acc[:],
-                lhsT=w_codes[0][:, 0:P].bitcast(FP8X4),
-                lhsT_scale=w_scales[0][:, 0:P],
-                rhs=w_codes[0][:].bitcast(FP8X4),
-                rhs_scale=w_scales[0][:],
-                start=True,
-                stop=True,
-            )
-
-        quantise_w(1)
+        own_turned = bank(5, [P, P])
+        nc.tensor.transpose(own_turned[:], own_rows[:], ident[:])
         gather_x(0, 0, S)
-        for lo, hi in X_PIECES:
-            gather_x(1, lo, hi)
+        quantise_w(0)
 
         turned = bank(4, [P, TILES, P])
         for b in range(V // P):
@@ -156,8 +143,6 @@ def tile_picked_ytani_sim_p_kernel(
         nc.scalar.copy(q_cols[:], turned[:, :, P - 1])
         own_first = placed("own_first", [P, 1], F32, 4096 + 128)
         own_rest = placed("own_rest", [P, TILES - 1], F32, 4096 + 64)
-        own_turned = bank(5, [P, P])
-        nc.tensor.transpose(own_turned[:], own_rows[:], ident[:])
         first = P - TILES
         nc.scalar.activation(own_first[:], own_turned[:, first : first + 1], ACT.Copy, scale=INV_GAIN)
         nc.scalar.activation(own_rest[:], own_turned[:, first + 1 : P], ACT.Copy, scale=INV_GAIN)
@@ -169,6 +154,28 @@ def tile_picked_ytani_sim_p_kernel(
             )
         q_all = placed("q_all", [P, V], F32, 0)
         nc.scalar.copy(q_all[:], spread[:])
+
+        h_accs = [bank(j, [P, PACK, P]) for j in range(TILES)]
+
+        def hidden_pass(j, o):
+            cols = slice(j * P, (j + 1) * P)
+            for t in range(PACK):
+                chans = slice(t * P, (t + 1) * P)
+                nc.tensor.matmul_mx(
+                    h_accs[j][:, t, :],
+                    lhsT=w_codes[o][:, chans].bitcast(FP8X4),
+                    lhsT_scale=w_scales[o][:, chans],
+                    rhs=xw[o][:, cols].bitcast(FP8X4),
+                    rhs_scale=xs[4 * o : P, cols],
+                    start=(o == 0 and t == 0),
+                    stop=(o == PASSES - 1 and t == PACK - 1),
+                )
+
+        for j in range(TILES):
+            hidden_pass(j, 0)
+        quantise_w(1)
+        for lo, hi in X_PIECES:
+            gather_x(1, lo, hi)
 
         ew = sbuf("ew", [P, V], U32)
         nc.vector.tensor_copy(ew[:], ew_win[:].bitcast(U32).indirect(refs_sb[:]))
@@ -182,20 +189,8 @@ def tile_picked_ytani_sim_p_kernel(
         h_grouped = {}
 
         def hidden(j):
-            cols = slice(j * P, (j + 1) * P)
-            h_acc = bank(j, [P, PACK, P])
-            for t in range(PACK):
-                chans = slice(t * P, (t + 1) * P)
-                for o in range(PASSES):
-                    nc.tensor.matmul_mx(
-                        h_acc[:, t, :],
-                        lhsT=w_codes[o][:, chans].bitcast(FP8X4),
-                        lhsT_scale=w_scales[o][:, chans],
-                        rhs=xw[o][:, cols].bitcast(FP8X4),
-                        rhs_scale=xs[4 * o : P, cols],
-                        start=(o == 0),
-                        stop=(o == PASSES - 1),
-                    )
+            hidden_pass(j, 1)
+            h_acc = h_accs[j]
             grouped = sbuf("h_grouped%d" % j, [P, P, PACK], BF16)
             nc.scalar.copy(grouped[:], h_acc[:].rearrange("p t n -> p n t"))
             h_grouped[j] = grouped
@@ -220,7 +215,7 @@ def tile_picked_ytani_sim_p_kernel(
             )
             return acc
 
-        accs, dens, signs, invs, signeds = {}, {}, {}, {}, {}
+        accs, dens, signs, invs, signeds, roots, units = {}, {}, {}, {}, {}, {}, {}
 
         def denominator(j):
             accs[j] = product(j)
@@ -229,46 +224,45 @@ def tile_picked_ytani_sim_p_kernel(
                 dens[j][:], q_all[:], own_cols[j], accs[j][:], ALU.add, ALU.subtract
             )
 
+        def sign(j):
+            signs[j] = sbuf("sign%d" % j, [P, V], F32)
+            nc.gpsimd.tensor_scalar(signs[j][:], dens[j][:], TINY, -TINY, ALU.min, ALU.max)
+            units[j] = 1.0 / TINY
+
         def sign_on_scalar(j):
             signs[j] = sbuf("sign%d" % j, [P, V], F32)
             nc.scalar.activation(signs[j][:], dens[j][:], ACT.Sign)
-            signeds[j] = 1.0
+            units[j] = 1.0
 
-        def sign_on_vector(j):
-            signs[j] = sbuf("sign%d" % j, [P, V], F32)
-            nc.vector.tensor_scalar(signs[j][:], dens[j][:], 0.0, 0.5, ALU.is_ge, ALU.subtract)
-            signeds[j] = 2.0
+        def root(j):
+            roots[j] = sbuf("root%d" % j, [P, V], F32)
+            nc.scalar.activation(roots[j][:], dens[j][:], ACT.Abs_reciprocal_sqrt)
+
+        def square(j, lo, hi):
+            if j not in invs:
+                invs[j] = sbuf("inv%d" % j, [P, V], F32)
+            nc.scalar.activation(invs[j][:, lo:hi], roots[j][:, lo:hi], ACT.Square)
 
         def inverse(j):
-            root = sbuf("root%d" % j, [P, V], F32)
-            nc.scalar.activation(root[:], dens[j][:], ACT.Abs_reciprocal_sqrt)
-            invs[j] = sbuf("inv%d" % j, [P, V], F32)
-            nc.scalar.activation(invs[j][:], root[:], ACT.Square)
+            root(j)
+            square(j, 0, V)
 
         def numerator(j):
-            factor = signeds[j]
             signeds[j] = sbuf("signed%d" % j, [P, V], F32)
             nc.vector.scalar_tensor_tensor(
-                signeds[j][:], accs[j][:], factor, signs[j][:], ALU.mult, ALU.mult
+                signeds[j][:], signs[j][:], units[j], accs[j][:], ALU.mult, ALU.mult
             )
 
-        def reciprocal_on_gpsimd(j):
-            invs[j, "signed"] = sbuf("recip%d" % j, [P, V], F32)
-            nc.gpsimd.tensor_tensor(invs[j, "signed"][:], signs[j][:], invs[j][:], ALU.mult)
+        results = {}
 
-        def finish_from_bank(j):
-            result = sbuf("result%d" % j, [P, V], F32)
-            nc.vector.scalar_tensor_tensor(
-                result[:], accs[j][:], signeds[j], invs[j, "signed"][:], ALU.mult, ALU.mult
-            )
-            nc.sync.dma_start(out[j * P : (j + 1) * P, :], result[:])
+        def finish(j, engine, lo, hi):
+            if j not in results:
+                results[j] = sbuf("result%d" % j, [P, V], F32)
+            part = slice(lo, hi)
+            engine.tensor_tensor(results[j][:, part], signeds[j][:, part], invs[j][:, part], ALU.mult)
 
-        def finish(j, engine, width):
-            result = sbuf("result%d" % j, [P, V], F32)
-            for lo in range(0, V, width):
-                part = slice(lo, lo + width)
-                engine.tensor_tensor(result[:, part], signeds[j][:, part], invs[j][:, part], ALU.mult)
-                nc.sync.dma_start(out[j * P : (j + 1) * P, part], result[:, part])
+        def store(j, lo, hi):
+            nc.sync.dma_start(out[j * P : (j + 1) * P, lo:hi], results[j][:, lo:hi])
 
         for j in range(TILES):
             hidden(j)
@@ -276,22 +270,29 @@ def tile_picked_ytani_sim_p_kernel(
             quantise_h(j)
         denominator(0)
         quantise_h(TILES - 1)
-        sign_on_vector(0)
+        sign(0)
         inverse(0)
         denominator(1)
-        sign_on_vector(1)
-        numerator(0)
+        sign(1)
         inverse(1)
-        finish(0, nc.gpsimd, V)
         denominator(2)
-        numerator(1)
-        sign_on_scalar(2)
-        inverse(2)
-        finish(1, nc.gpsimd, V)
+        sign(2)
+        root(2)
+        numerator(0)
+        finish(0, nc.gpsimd, 0, V)
+        store(0, 0, V)
         denominator(3)
-        numerator(2)
         sign_on_scalar(3)
-        inverse(3)
-        finish(2, nc.gpsimd, V)
+        square(2, 0, V)
+        root(3)
+        numerator(1)
+        finish(1, nc.gpsimd, 0, V)
+        store(1, 0, V)
+        numerator(2)
         numerator(3)
-        finish(3, nc.vector, V // 2)
+        finish(2, nc.vector, 0, V)
+        store(2, 0, V)
+        for lo in range(0, V, V // 2):
+            square(3, lo, lo + V // 2)
+            finish(3, nc.vector, lo, lo + V // 2)
+            store(3, lo, lo + V // 2)

@@ -23,6 +23,7 @@ PASSES = K // (P * PACK)
 TILES = S // P
 INV_GAIN = 1.0 / 0.3
 VECTOR_SHARE = (16, 84)
+GPSIMD_PART = 320
 TINY = 2.0 ** -120
 X_PIECES = ((0, 128), (128, 256), (256, 512))
 
@@ -94,9 +95,7 @@ def tile_picked_ytani_sim_p_kernel(
         nc.sync.dma_start(ew_win[:], e_words[0].rearrange("p n t -> p (n t)").bitcast(I32))
 
         q_row = sbuf("q_row", [P, V], F32)
-        nc.vector.tensor_scalar(
-            q_row[:], qn_win[:].indirect(refs_sb[:]), INV_GAIN, 0.0, ALU.mult, ALU.add
-        )
+        nc.vector.tensor_copy(q_row[:], qn_win[:].indirect(refs_sb[:]))
         xs = sbuf("xs", [P, S], U8)
         nc.vector.tensor_copy(xs[:], xs_win[:].indirect(offs_sb[:]))
         es_picked = sbuf("es_picked", [P, V], U8)
@@ -140,7 +139,7 @@ def tile_picked_ytani_sim_p_kernel(
         for b in range(V // P):
             nc.tensor.transpose(turned[:, b, :], q_row[:, b * P : (b + 1) * P], ident[:])
         q_cols = sbuf("q_cols", [P, V // P], F32)
-        nc.scalar.copy(q_cols[:], turned[:, :, P - 1])
+        nc.scalar.activation(q_cols[:], turned[:, :, P - 1], ACT.Copy, scale=INV_GAIN)
         own_first = placed("own_first", [P, 1], F32, 4096 + 128)
         own_rest = placed("own_rest", [P, TILES - 1], F32, 4096 + 64)
         first = P - TILES
@@ -286,10 +285,12 @@ def tile_picked_ytani_sim_p_kernel(
         square(2, 0, V)
         root(3)
         numerator(1)
-        finish(1, nc.gpsimd, 0, V)
-        store(1, 0, V)
+        finish(1, nc.gpsimd, 0, GPSIMD_PART)
+        store(1, 0, GPSIMD_PART)
         numerator(2)
         numerator(3)
+        finish(1, nc.vector, GPSIMD_PART, V)
+        store(1, GPSIMD_PART, V)
         finish(2, nc.vector, 0, V)
         store(2, 0, V)
         for lo in range(0, V, V // 2):

@@ -65,7 +65,7 @@ def tile_picked_ytani_sim_p_kernel(
         nc.gpsimd.memset(es[:].bitcast(I32), 0)
         nc.scalar.activation(warm[:, 1:2], warm[:, 0:1], ACT.Abs_reciprocal_sqrt)
 
-        w_raw = [placed("w_raw0", [P, PACK, H], F32, 0), sbuf("w_raw1", [P, PACK, H], F32)]
+        w_raw = [placed("w_raw0", [P, PACK, H], F32, 0), placed("w_raw1", [P, PACK, H], F32, 8192)]
         xw_win = [sbuf("xw_win%d" % o, [P, T], I32) for o in range(PASSES)]
         ew_win = sbuf("ew_win", [P, W], I32)
 
@@ -140,19 +140,20 @@ def tile_picked_ytani_sim_p_kernel(
             nc.tensor.transpose(turned[:, b, :], q_row[:, b * P : (b + 1) * P], ident[:])
         q_cols = sbuf("q_cols", [P, V // P], F32)
         nc.scalar.activation(q_cols[:], turned[:, :, P - 1], ACT.Copy, scale=INV_GAIN)
-        own_first = placed("own_first", [P, 1], F32, 4096 + 128)
-        own_rest = placed("own_rest", [P, TILES - 1], F32, 4096 + 64)
-        first = P - TILES
-        nc.scalar.activation(own_first[:], own_turned[:, first : first + 1], ACT.Copy, scale=INV_GAIN)
-        nc.scalar.activation(own_rest[:], own_turned[:, first + 1 : P], ACT.Copy, scale=INV_GAIN)
-        own_cols = [own_first[:]] + [own_rest[:, j : j + 1] for j in range(TILES - 1)]
+        own_cols = placed("own_cols", [P, TILES], F32, 4096)
+        nc.scalar.activation(own_cols[:], own_turned[:, P - TILES : P], ACT.Copy, scale=INV_GAIN)
         spread = bank(6, [P, V])
         for b in range(V // P):
             nc.tensor.transpose(
                 spread[:, b * P : (b + 1) * P], q_cols[:, b : b + 1].to_broadcast([P, P]), ident[:]
             )
-        q_all = placed("q_all", [P, V], F32, 0)
-        nc.scalar.copy(q_all[:], spread[:])
+        norms = {}
+
+        def add_norms(j, offset):
+            norms[j] = placed("norms%d" % j, [P, V], F32, offset)
+            nc.scalar.activation(norms[j][:], spread[:], ACT.Identity, bias=own_cols[:, j : j + 1])
+
+        add_norms(0, 0)
 
         h_accs = [bank(j, [P, PACK, P]) for j in range(TILES)]
 
@@ -173,6 +174,8 @@ def tile_picked_ytani_sim_p_kernel(
         for j in range(TILES):
             hidden_pass(j, 0)
         quantise_w(1)
+        for j in range(1, TILES):
+            add_norms(j, 8192 + 2048 * j)
         for lo, hi in X_PIECES:
             gather_x(1, lo, hi)
 
@@ -182,7 +185,7 @@ def tile_picked_ytani_sim_p_kernel(
         h_words = sbuf("h_words", [P, S], U32, tag="es_picked")
         h_codes = [h_words[:, j * P : (j + 1) * P] for j in range(TILES)]
         h_scales_early = sbuf("h_scales_early", [P, S - P], U8)
-        h_scales_last = placed("h_scales_last", [P, P], U8, 4096 + 128)
+        h_scales_last = placed("h_scales_last", [P, P], U8, 0)
         h_scales = [h_scales_early[:, j * P : (j + 1) * P] for j in range(TILES - 1)]
         h_scales.append(h_scales_last[:])
         h_grouped = {}
@@ -219,9 +222,7 @@ def tile_picked_ytani_sim_p_kernel(
         def denominator(j):
             accs[j] = product(j)
             dens[j] = sbuf("den%d" % j, [P, V], F32)
-            nc.vector.scalar_tensor_tensor(
-                dens[j][:], q_all[:], own_cols[j], accs[j][:], ALU.add, ALU.subtract
-            )
+            nc.vector.tensor_tensor(dens[j][:], norms[j][:], accs[j][:], ALU.subtract)
 
         def sign(j):
             signs[j] = sbuf("sign%d" % j, [P, V], F32)

@@ -185,7 +185,7 @@ def tile_picked_ytani_sim_p_kernel(
         h_words = sbuf("h_words", [P, S], U32, tag="es_picked")
         h_codes = [h_words[:, j * P : (j + 1) * P] for j in range(TILES)]
         h_scales_early = sbuf("h_scales_early", [P, S - P], U8)
-        h_scales_last = placed("h_scales_last", [P, P], U8, 0)
+        h_scales_last = placed("h_scales_last", [P, P], U8, 1024)
         h_scales = [h_scales_early[:, j * P : (j + 1) * P] for j in range(TILES - 1)]
         h_scales.append(h_scales_last[:])
         h_grouped = {}
@@ -219,10 +219,12 @@ def tile_picked_ytani_sim_p_kernel(
 
         accs, dens, signs, invs, signeds, roots, units = {}, {}, {}, {}, {}, {}, {}
 
-        def denominator(j):
+        def denominator(j, width=V):
             accs[j] = product(j)
             dens[j] = sbuf("den%d" % j, [P, V], F32)
-            nc.vector.tensor_tensor(dens[j][:], norms[j][:], accs[j][:], ALU.subtract)
+            for lo in range(0, V, width):
+                part = slice(lo, lo + width)
+                nc.vector.tensor_tensor(dens[j][:, part], norms[j][:, part], accs[j][:, part], ALU.subtract)
 
         def sign(j):
             signs[j] = sbuf("sign%d" % j, [P, V], F32)
@@ -234,9 +236,11 @@ def tile_picked_ytani_sim_p_kernel(
             nc.scalar.activation(signs[j][:], dens[j][:], ACT.Sign)
             units[j] = 1.0
 
-        def root(j):
+        def root(j, width=V):
             roots[j] = sbuf("root%d" % j, [P, V], F32)
-            nc.scalar.activation(roots[j][:], dens[j][:], ACT.Abs_reciprocal_sqrt)
+            for lo in range(0, V, width):
+                part = slice(lo, lo + width)
+                nc.scalar.activation(roots[j][:, part], dens[j][:, part], ACT.Abs_reciprocal_sqrt)
 
         def square(j, lo, hi):
             if j not in invs:
@@ -268,11 +272,12 @@ def tile_picked_ytani_sim_p_kernel(
             hidden(j)
         for j in range(TILES - 1):
             quantise_h(j)
-        denominator(0)
-        quantise_h(TILES - 1)
+        denominator(0, V // 2)
         sign(0)
-        inverse(0)
+        root(0, V // 2)
+        square(0, 0, V)
         denominator(1)
+        quantise_h(TILES - 1)
         sign(1)
         inverse(1)
         denominator(2)

@@ -21,6 +21,7 @@ P = 128
 PACK = 4
 PASSES = K // (P * PACK)
 TILES = S // P
+SCALE_ROWS = 16
 INV_GAIN = 1.0 / 0.3
 VECTOR_SHARE = (16, 84)
 GPSIMD_PART = 320
@@ -56,7 +57,7 @@ def tile_picked_ytani_sim_p_kernel(
         warm = sbuf("warm", [P, 2], F32)
 
         nc.gpsimd.memset(xs_win[:].bitcast(I32), 0)
-        nc.gpsimd.memset(es_win[:].bitcast(I32), 0)
+        nc.gpsimd.memset(es_win[0 : P - SCALE_ROWS, :].bitcast(I32), 0)
         nc.vector.memset(warm[:, 0:1], 1.0)
         nc.vector.memset(qn_win[0 : P - 1, :].bitcast(I32), 0)
         nc.gpsimd.memset(own_rows[0 : P - TILES, :], 0.0)
@@ -81,13 +82,13 @@ def tile_picked_ytani_sim_p_kernel(
         nc.sync.dma_start(refs_sb[:], refs)
         nc.sync.dma_start(qn_win[P - 1 : P, :], qn[0:1, :])
         nc.sync.dma_start(offs_sb[:], offs)
+        nc.sync.dma_start(es_win[P - SCALE_ROWS : P, :].bitcast(I32), e_scales[0].bitcast(I32))
+        load_w(0)
         for q in range(4):
             nc.sync.dma_start(
                 xs_win[32 * q : 32 * q + 4 * PASSES, :].bitcast(I32),
                 x_scales[:, 4 * q : 4 * q + 4, :].bitcast(I32),
             )
-        load_w(0)
-        nc.sync.dma_start(es_win[0:P:8, :].bitcast(I32), e_scales[0].bitcast(I32))
         load_x(0)
         nc.sync.dma_start(own_rows[P - TILES : P, :], own.rearrange("(j p) o -> j (p o)", p=P))
         load_w(1)
@@ -96,15 +97,16 @@ def tile_picked_ytani_sim_p_kernel(
 
         q_row = sbuf("q_row", [P, V], F32)
         nc.vector.tensor_copy(q_row[:], qn_win[:].indirect(refs_sb[:]))
-        xs = sbuf("xs", [P, S], U8)
-        nc.vector.tensor_copy(xs[:], xs_win[:].indirect(offs_sb[:]))
         es_picked = sbuf("es_picked", [P, V], U8)
         nc.vector.tensor_copy(es_picked[:], es_win[:].indirect(refs_sb[:]))
         for q in range(4):
             nc.sync.dma_start(
                 es[32 * q : 32 * q + 4, :].bitcast(I32),
-                es_picked[32 * q : 32 * q + 32 : 8, :].bitcast(I32),
+                es_picked[P - SCALE_ROWS + 4 * q : P - SCALE_ROWS + 4 * q + 4, :].bitcast(I32),
             )
+
+        xs = sbuf("xs", [P, S], U8)
+        nc.vector.tensor_copy(xs[:], xs_win[:].indirect(offs_sb[:]))
 
         xw = [sbuf("xw%d" % o, [P, S], U32) for o in range(PASSES)]
 
@@ -117,7 +119,7 @@ def tile_picked_ytani_sim_p_kernel(
         w_codes, w_scales = [], []
 
         def quantise_w(o):
-            grouped = sbuf("w_grouped%d" % o, [P, PACK * H], BF16)
+            grouped = sbuf("w_grouped%d" % o, [P, PACK * H], BF16, tag="q_row" if o == 0 else None)
             src = w_raw[o][:].rearrange("p j (m t) -> p m j t", t=PACK)
             dst = grouped[:].rearrange("p (t m j) -> p m j t", t=PACK, j=PACK)
             cut = P - VECTOR_SHARE[o]
@@ -130,16 +132,16 @@ def tile_picked_ytani_sim_p_kernel(
             w_codes.append(codes)
             w_scales.append(scales)
 
-        own_turned = bank(5, [P, P])
-        nc.tensor.transpose(own_turned[:], own_rows[:], ident[:])
-        gather_x(0, 0, S)
-        quantise_w(0)
-
         turned = bank(4, [P, TILES, P])
         for b in range(V // P):
             nc.tensor.transpose(turned[:, b, :], q_row[:, b * P : (b + 1) * P], ident[:])
         q_cols = sbuf("q_cols", [P, V // P], F32)
         nc.scalar.activation(q_cols[:], turned[:, :, P - 1], ACT.Copy, scale=INV_GAIN)
+        own_turned = bank(5, [P, P])
+        nc.tensor.transpose(own_turned[:], own_rows[:], ident[:])
+        gather_x(0, 0, S)
+        quantise_w(0)
+
         own_cols = placed("own_cols", [P, TILES], F32, 4096)
         nc.scalar.activation(own_cols[:], own_turned[:, P - TILES : P], ACT.Copy, scale=INV_GAIN)
         spread = bank(6, [P, V])

@@ -22,6 +22,7 @@ PACK = 4
 PASSES = K // (P * PACK)
 TILES = S // P
 SCALE_ROWS = 16
+ES_FIRST = 48
 INV_GAIN = 1.0 / 0.3
 VECTOR_SHARE = (16, 84)
 GPSIMD_PART = 320
@@ -57,7 +58,8 @@ def tile_picked_ytani_sim_p_kernel(
         warm = sbuf("warm", [P, 2], F32)
 
         nc.gpsimd.memset(xs_win[:].bitcast(I32), 0)
-        nc.gpsimd.memset(es_win[0 : P - SCALE_ROWS, :].bitcast(I32), 0)
+        nc.gpsimd.memset(es_win[0:ES_FIRST, :].bitcast(I32), 0)
+        nc.gpsimd.memset(es_win[ES_FIRST + SCALE_ROWS : P, :].bitcast(I32), 0)
         nc.vector.memset(warm[:, 0:1], 1.0)
         nc.vector.memset(qn_win[0 : P - 1, :].bitcast(I32), 0)
         nc.gpsimd.memset(own_rows[0 : P - TILES, :], 0.0)
@@ -79,10 +81,10 @@ def tile_picked_ytani_sim_p_kernel(
                 xw_win[o][:], x_words[o].rearrange("p n t -> p (n t)").bitcast(I32)
             )
 
-        nc.sync.dma_start(refs_sb[:], refs)
         nc.sync.dma_start(qn_win[P - 1 : P, :], qn[0:1, :])
+        nc.sync.dma_start(es_win[ES_FIRST : ES_FIRST + SCALE_ROWS, :].bitcast(I32), e_scales[0].bitcast(I32))
+        nc.sync.dma_start(refs_sb[:], refs)
         nc.sync.dma_start(offs_sb[:], offs)
-        nc.sync.dma_start(es_win[P - SCALE_ROWS : P, :].bitcast(I32), e_scales[0].bitcast(I32))
         load_w(0)
         for q in range(4):
             nc.sync.dma_start(
@@ -102,7 +104,7 @@ def tile_picked_ytani_sim_p_kernel(
         for q in range(4):
             nc.sync.dma_start(
                 es[32 * q : 32 * q + 4, :].bitcast(I32),
-                es_picked[P - SCALE_ROWS + 4 * q : P - SCALE_ROWS + 4 * q + 4, :].bitcast(I32),
+                es_picked[ES_FIRST + 4 * q : ES_FIRST + 4 * q + 4, :].bitcast(I32),
             )
 
         xs = sbuf("xs", [P, S], U8)

@@ -25,7 +25,7 @@ SCALE_ROWS = 16
 ES_FIRST = 48
 INV_GAIN = 1.0 / 0.3
 VECTOR_SHARE = (16, 84)
-GPSIMD_PART = 320
+GPSIMD_PART = 416
 TINY = 2.0 ** -120
 X_PIECES = ((0, 128), (128, 256), (256, 512))
 
@@ -153,11 +153,12 @@ def tile_picked_ytani_sim_p_kernel(
             )
         norms = {}
 
-        def add_norms(j, offset):
-            norms[j] = placed("norms%d" % j, [P, V], F32, offset)
-            nc.scalar.activation(norms[j][:], spread[:], ACT.Identity, bias=own_cols[:, j : j + 1])
+        def add_norms(j, offset, lo=0, hi=V):
+            norms[j, lo] = placed("norms%d_%d" % (j, lo), [P, hi - lo], F32, offset + 4 * lo)
+            nc.scalar.activation(norms[j, lo][:], spread[:, lo:hi], ACT.Identity, bias=own_cols[:, j : j + 1])
 
-        add_norms(0, 0)
+        add_norms(0, 0, 0, V // 2)
+        add_norms(0, 0, V // 2, V)
 
         h_accs = [bank(j, [P, PACK, P]) for j in range(TILES)]
 
@@ -189,7 +190,7 @@ def tile_picked_ytani_sim_p_kernel(
         h_words = sbuf("h_words", [P, S], U32, tag="es_picked")
         h_codes = [h_words[:, j * P : (j + 1) * P] for j in range(TILES)]
         h_scales_early = sbuf("h_scales_early", [P, S - P], U8)
-        h_scales_last = placed("h_scales_last", [P, P], U8, 1024)
+        h_scales_last = placed("h_scales_last", [P, P], U8, 0)
         h_scales = [h_scales_early[:, j * P : (j + 1) * P] for j in range(TILES - 1)]
         h_scales.append(h_scales_last[:])
         h_grouped = {}
@@ -228,17 +229,25 @@ def tile_picked_ytani_sim_p_kernel(
             dens[j] = sbuf("den%d" % j, [P, V], F32)
             for lo in range(0, V, width):
                 part = slice(lo, lo + width)
-                nc.vector.tensor_tensor(dens[j][:, part], norms[j][:, part], accs[j][:, part], ALU.subtract)
+                nc.vector.tensor_tensor(dens[j][:, part], norms[j, lo][:], accs[j][:, part], ALU.subtract)
 
-        def sign(j):
+        def sign(j, width=V):
             signs[j] = sbuf("sign%d" % j, [P, V], F32)
-            nc.gpsimd.tensor_scalar(signs[j][:], dens[j][:], TINY, -TINY, ALU.min, ALU.max)
+            for lo in range(0, V, width):
+                part = slice(lo, lo + width)
+                nc.gpsimd.tensor_scalar(signs[j][:, part], dens[j][:, part], TINY, -TINY, ALU.min, ALU.max)
             units[j] = 1.0 / TINY
 
         def sign_on_scalar(j):
             signs[j] = sbuf("sign%d" % j, [P, V], F32)
             nc.scalar.activation(signs[j][:], dens[j][:], ACT.Sign)
             units[j] = 1.0
+
+        def sign_shared(j):
+            signs[j] = sbuf("sign%d" % j, [P, V], F32)
+            nc.gpsimd.tensor_scalar(signs[j][:, 0 : V // 2], dens[j][:, 0 : V // 2], TINY, -TINY, ALU.min, ALU.max)
+            nc.scalar.activation(signs[j][:, V // 2 : V], dens[j][:, V // 2 : V], ACT.Sign)
+            units[j] = None
 
         def root(j, width=V):
             roots[j] = sbuf("root%d" % j, [P, V], F32)
@@ -252,14 +261,17 @@ def tile_picked_ytani_sim_p_kernel(
             nc.scalar.activation(invs[j][:, lo:hi], roots[j][:, lo:hi], ACT.Square)
 
         def inverse(j):
-            root(j)
-            square(j, 0, V)
+            root(j, V // 2)
+            square(j, 0, V // 2)
+            square(j, V // 2, V)
 
         def numerator(j):
             signeds[j] = sbuf("signed%d" % j, [P, V], F32)
-            nc.vector.scalar_tensor_tensor(
-                signeds[j][:], signs[j][:], units[j], accs[j][:], ALU.mult, ALU.mult
-            )
+            parts = [(0, V, units[j])] if units[j] else [(0, V // 2, 1.0 / TINY), (V // 2, V, 1.0)]
+            for lo, hi, unit in parts:
+                nc.vector.scalar_tensor_tensor(
+                    signeds[j][:, lo:hi], signs[j][:, lo:hi], unit, accs[j][:, lo:hi], ALU.mult, ALU.mult
+                )
 
         results = {}
 
@@ -277,15 +289,14 @@ def tile_picked_ytani_sim_p_kernel(
         for j in range(TILES - 1):
             quantise_h(j)
         denominator(0, V // 2)
-        sign(0)
-        root(0, V // 2)
-        square(0, 0, V)
-        denominator(1)
         quantise_h(TILES - 1)
+        sign(0)
+        inverse(0)
+        denominator(1)
         sign(1)
         inverse(1)
         denominator(2)
-        sign(2)
+        sign_shared(2)
         root(2)
         numerator(0)
         finish(0, nc.gpsimd, 0, V)
@@ -293,7 +304,7 @@ def tile_picked_ytani_sim_p_kernel(
         denominator(3)
         sign_on_scalar(3)
         square(2, 0, V)
-        root(3)
+        root(3, V // 2)
         numerator(1)
         finish(1, nc.gpsimd, 0, GPSIMD_PART)
         store(1, 0, GPSIMD_PART)

@@ -25,6 +25,7 @@ SCALE_ROWS = 16
 ES_FIRST = 48
 INV_GAIN = 1.0 / 0.3
 VECTOR_SHARE = (16, 84)
+VECTOR_CLEARS = 1536
 GPSIMD_PART = 416
 TINY = 2.0 ** -120
 X_PIECES = ((0, 128), (128, 256), (256, 512))
@@ -58,10 +59,11 @@ def tile_picked_ytani_sim_p_kernel(
         warm = sbuf("warm", [P, 2], F32)
 
         nc.gpsimd.memset(xs_win[:].bitcast(I32), 0)
+        nc.gpsimd.memset(qn_win[0 : P - 1, VECTOR_CLEARS:W].bitcast(I32), 0)
         nc.gpsimd.memset(es_win[0:ES_FIRST, :].bitcast(I32), 0)
         nc.gpsimd.memset(es_win[ES_FIRST + SCALE_ROWS : P, :].bitcast(I32), 0)
         nc.vector.memset(warm[:, 0:1], 1.0)
-        nc.vector.memset(qn_win[0 : P - 1, :].bitcast(I32), 0)
+        nc.vector.memset(qn_win[0 : P - 1, 0:VECTOR_CLEARS].bitcast(I32), 0)
         nc.gpsimd.memset(own_rows[0 : P - TILES, :], 0.0)
         make_identity(nc, ident[:])
         es = sbuf("es", [P, V], U8)
@@ -99,7 +101,7 @@ def tile_picked_ytani_sim_p_kernel(
 
         q_row = sbuf("q_row", [P, V], F32)
         nc.vector.tensor_copy(q_row[:], qn_win[:].indirect(refs_sb[:]))
-        es_picked = sbuf("es_picked", [P, V], U8)
+        es_picked = placed("es_picked", [P, V], U8, 16384 + 1792)
         nc.vector.tensor_copy(es_picked[:], es_win[:].indirect(refs_sb[:]))
         for q in range(4):
             nc.sync.dma_start(
@@ -184,10 +186,13 @@ def tile_picked_ytani_sim_p_kernel(
         for lo, hi in X_PIECES:
             gather_x(1, lo, hi)
 
-        ew = sbuf("ew", [P, V], U32)
-        nc.vector.tensor_copy(ew[:], ew_win[:].bitcast(U32).indirect(refs_sb[:]))
+        ew = [sbuf("ew0", [P, V // 2], U32), placed("ew1", [P, V // 2], U32, 16384 + 2048)]
 
-        h_words = sbuf("h_words", [P, S], U32, tag="es_picked")
+        def gather_e(half):
+            offsets = refs_sb[:, half * V // 32 : (half + 1) * V // 32]
+            nc.vector.tensor_copy(ew[half][:], ew_win[:].bitcast(U32).indirect(offsets))
+
+        h_words = placed("h_words", [P, S], U32, 16384)
         h_codes = [h_words[:, j * P : (j + 1) * P] for j in range(TILES)]
         h_scales_early = sbuf("h_scales_early", [P, S - P], U8)
         h_scales_last = placed("h_scales_last", [P, P], U8, 0)
@@ -209,27 +214,36 @@ def tile_picked_ytani_sim_p_kernel(
                 h_grouped[j][:].rearrange("p n t -> p (n t)"),
             )
 
-        def product(j):
-            acc = bank(TILES + j, [P, V])
+        def product(j, half, acc):
             nc.tensor.matmul_mx(
-                acc[:],
+                acc,
                 lhsT=h_codes[j].bitcast(FP8X4),
                 lhsT_scale=h_scales[j],
-                rhs=ew[:].bitcast(FP8X4),
-                rhs_scale=es[:],
+                rhs=ew[half][:].bitcast(FP8X4),
+                rhs_scale=es[:, half * V // 2 : (half + 1) * V // 2],
                 start=True,
                 stop=True,
             )
-            return acc
+
+        def products(j):
+            if j == 0:
+                halves = [bank(TILES, [P, V // 2]), bank(0, [P, V // 2])]
+                parts = [(half * V // 2, (half + 1) * V // 2, halves[half][:]) for half in range(2)]
+                for half in range(2):
+                    product(j, half, halves[half][:])
+                return parts
+            acc = bank(TILES + j, [P, V])
+            for half in range(2):
+                product(j, half, acc[:, half * V // 2 : (half + 1) * V // 2])
+            return [(0, V, acc[:])]
 
         accs, dens, signs, invs, signeds, roots, units = {}, {}, {}, {}, {}, {}, {}
 
-        def denominator(j, width=V):
-            accs[j] = product(j)
+        def denominator(j):
+            accs[j] = products(j)
             dens[j] = sbuf("den%d" % j, [P, V], F32)
-            for lo in range(0, V, width):
-                part = slice(lo, lo + width)
-                nc.vector.tensor_tensor(dens[j][:, part], norms[j, lo][:], accs[j][:, part], ALU.subtract)
+            for lo, hi, acc in accs[j]:
+                nc.vector.tensor_tensor(dens[j][:, lo:hi], norms[j, lo][:], acc, ALU.subtract)
 
         def sign(j, width=V):
             signs[j] = sbuf("sign%d" % j, [P, V], F32)
@@ -267,10 +281,14 @@ def tile_picked_ytani_sim_p_kernel(
 
         def numerator(j):
             signeds[j] = sbuf("signed%d" % j, [P, V], F32)
-            parts = [(0, V, units[j])] if units[j] else [(0, V // 2, 1.0 / TINY), (V // 2, V, 1.0)]
-            for lo, hi, unit in parts:
+            if units[j]:
+                parts = [(lo, hi, acc, units[j]) for lo, hi, acc in accs[j]]
+            else:
+                acc = accs[j][0][2]
+                parts = [(0, V // 2, acc[:, 0 : V // 2], 1.0 / TINY), (V // 2, V, acc[:, V // 2 : V], 1.0)]
+            for lo, hi, acc, unit in parts:
                 nc.vector.scalar_tensor_tensor(
-                    signeds[j][:, lo:hi], signs[j][:, lo:hi], unit, accs[j][:, lo:hi], ALU.mult, ALU.mult
+                    signeds[j][:, lo:hi], signs[j][:, lo:hi], unit, acc, ALU.mult, ALU.mult
                 )
 
         results = {}
@@ -286,9 +304,12 @@ def tile_picked_ytani_sim_p_kernel(
 
         for j in range(TILES):
             hidden(j)
-        for j in range(TILES - 1):
+        gather_e(0)
+        quantise_h(0)
+        gather_e(1)
+        for j in range(1, TILES - 1):
             quantise_h(j)
-        denominator(0, V // 2)
+        denominator(0)
         quantise_h(TILES - 1)
         sign(0)
         inverse(0)

@@ -26,7 +26,7 @@ ES_FIRST = 48
 INV_GAIN = 1.0 / 0.3
 VECTOR_SHARE = (16, 84)
 VECTOR_CLEARS = 1536
-GPSIMD_PART = 416
+GPSIMD_PART = 384
 TINY = 2.0 ** -120
 X_PIECES = ((0, 128), (128, 256), (256, 512))
 
@@ -259,7 +259,8 @@ def tile_picked_ytani_sim_p_kernel(
 
         def sign_shared(j):
             signs[j] = sbuf("sign%d" % j, [P, V], F32)
-            nc.gpsimd.tensor_scalar(signs[j][:, 0 : V // 2], dens[j][:, 0 : V // 2], TINY, -TINY, ALU.min, ALU.max)
+            acc = accs[j][0][2]
+            nc.vector.tensor_tensor(signs[j][:, 0 : V // 2], norms[j, 0][:, 0 : V // 2], acc[:, 0 : V // 2], ALU.is_gt)
             nc.scalar.activation(signs[j][:, V // 2 : V], dens[j][:, V // 2 : V], ACT.Sign)
             units[j] = None
 
@@ -267,7 +268,8 @@ def tile_picked_ytani_sim_p_kernel(
             roots[j] = sbuf("root%d" % j, [P, V], F32)
             for lo in range(0, V, width):
                 part = slice(lo, lo + width)
-                nc.scalar.activation(roots[j][:, part], dens[j][:, part], ACT.Abs_reciprocal_sqrt)
+                scale = 0.5 if units[j] is None and lo == 0 else 1.0
+                nc.scalar.activation(roots[j][:, part], dens[j][:, part], ACT.Abs_reciprocal_sqrt, scale=scale)
 
         def square(j, lo, hi):
             if j not in invs:
@@ -282,14 +284,15 @@ def tile_picked_ytani_sim_p_kernel(
         def numerator(j):
             signeds[j] = sbuf("signed%d" % j, [P, V], F32)
             if units[j]:
-                parts = [(lo, hi, acc, units[j]) for lo, hi, acc in accs[j]]
+                parts = [(lo, hi, acc, units[j], ALU.mult) for lo, hi, acc in accs[j]]
             else:
                 acc = accs[j][0][2]
-                parts = [(0, V // 2, acc[:, 0 : V // 2], 1.0 / TINY), (V // 2, V, acc[:, V // 2 : V], 1.0)]
-            for lo, hi, acc, unit in parts:
-                nc.vector.scalar_tensor_tensor(
-                    signeds[j][:, lo:hi], signs[j][:, lo:hi], unit, acc, ALU.mult, ALU.mult
-                )
+                parts = [
+                    (0, V // 2, acc[:, 0 : V // 2], 0.5, ALU.subtract),
+                    (V // 2, V, acc[:, V // 2 : V], 1.0, ALU.mult),
+                ]
+            for lo, hi, acc, unit, op in parts:
+                nc.vector.scalar_tensor_tensor(signeds[j][:, lo:hi], signs[j][:, lo:hi], unit, acc, op, ALU.mult)
 
         results = {}
 
@@ -317,18 +320,18 @@ def tile_picked_ytani_sim_p_kernel(
         sign(1)
         inverse(1)
         denominator(2)
-        sign_shared(2)
+        sign_on_scalar(2)
         root(2)
         numerator(0)
         finish(0, nc.gpsimd, 0, V)
         store(0, 0, V)
         denominator(3)
-        sign_on_scalar(3)
-        square(2, 0, V)
-        root(3, V // 2)
         numerator(1)
         finish(1, nc.gpsimd, 0, GPSIMD_PART)
         store(1, 0, GPSIMD_PART)
+        sign_shared(3)
+        square(2, 0, V)
+        root(3, V // 2)
         numerator(2)
         numerator(3)
         finish(1, nc.vector, GPSIMD_PART, V)

@@ -97,13 +97,14 @@ def tile_picked_ytani_sim_p_kernel(
         nc.sync.dma_start(own_rows[P - TILES : P, :], own.rearrange("(j p) o -> j (p o)", p=P))
         load_w(1)
         load_x(1)
-        nc.sync.dma_start(ew_win[:], e_words[0].rearrange("p n t -> p (n t)").bitcast(I32))
 
         q_row = sbuf("q_row", [P, V], F32)
         nc.vector.tensor_copy(q_row[:], qn_win[:].indirect(refs_sb[:]))
         es_picked = placed("es_picked", [P, V], U8, 16384 + 1792)
         nc.vector.tensor_copy(es_picked[:], es_win[:].indirect(refs_sb[:]))
         for q in range(4):
+            if q == 3:
+                nc.sync.dma_start(ew_win[:], e_words[0].rearrange("p n t -> p (n t)").bitcast(I32))
             nc.sync.dma_start(
                 es[32 * q : 32 * q + 4, :].bitcast(I32),
                 es_picked[ES_FIRST + 4 * q : ES_FIRST + 4 * q + 4, :].bitcast(I32),

@@ -40,11 +40,11 @@ def tile_picked_ytani_sim_p_kernel(
         shared = ctx.enter_context(tc.tile_pool(name="shared", bufs=1))
         psum = ctx.enter_context(tc.psum_pool(name="psum", bufs=1))
 
-        def sbuf(name, shape, dtype, tag=None):
-            return keep.tile(shape, dtype, name=name, tag=tag or name, align_bytes=64)
+        def sbuf(name, shape, dtype, tag=None, align=64):
+            return keep.tile(shape, dtype, name=name, tag=tag or name, align_bytes=align)
 
-        def placed(name, shape, dtype, offset):
-            return shared.tile(shape, dtype, name=name, offset=offset, align_bytes=64)
+        def placed(name, shape, dtype, offset, align=64):
+            return shared.tile(shape, dtype, name=name, offset=offset, align_bytes=align)
 
         def bank(number, shape):
             return psum.tile(shape, F32, name="bank%d" % number)
@@ -70,9 +70,9 @@ def tile_picked_ytani_sim_p_kernel(
         nc.gpsimd.memset(es[:].bitcast(I32), 0)
         nc.scalar.activation(warm[:, 1:2], warm[:, 0:1], ACT.Abs_reciprocal_sqrt)
 
-        w_raw = [placed("w_raw0", [P, PACK, H], F32, 0), placed("w_raw1", [P, PACK, H], F32, 8192)]
-        xw_win = [sbuf("xw_win%d" % o, [P, T], I32) for o in range(PASSES)]
-        ew_win = sbuf("ew_win", [P, W], I32)
+        w_raw = [placed("w_raw0", [P, PACK, H], F32, 0, 256), placed("w_raw1", [P, PACK, H], F32, 8192, 256)]
+        xw_win = [sbuf("xw_win%d" % o, [P, T], I32, align=256) for o in range(PASSES)]
+        ew_win = sbuf("ew_win", [P, W], I32, align=256)
 
         def load_w(o):
             rows = w1[o * P * PACK : (o + 1) * P * PACK, :]
@@ -299,7 +299,7 @@ def tile_picked_ytani_sim_p_kernel(
 
         def finish(j, engine, lo, hi):
             if j not in results:
-                results[j] = sbuf("result%d" % j, [P, V], F32)
+                results[j] = sbuf("result%d" % j, [P, V], F32, align=256)
             part = slice(lo, hi)
             engine.tensor_tensor(results[j][:, part], signeds[j][:, part], invs[j][:, part], ALU.mult)
 

from contextlib import ExitStack

import concourse.mybir as mybir
from concourse.masks import make_identity

K, T, S, H, V, W = 1024, 1024, 512, 512, 512, 2048
FLOPS = 2 * K * H * S + 2 * H * S * V
BYTES = K * T + K * T // 32 + 4 * K * H + H * W + H * W // 32 + 4 * W + 4 * S + 2 * 2 * 128 * 32 + 4 * S * V

F32 = mybir.dt.float32
BF16 = mybir.dt.bfloat16
I32 = mybir.dt.int32
U32 = mybir.dt.uint32
U16 = mybir.dt.uint16
U8 = mybir.dt.uint8
FP8X4 = mybir.dt.float8_e4m3fn_x4
ALU = mybir.AluOpType
ACT = mybir.ActivationFunctionType

P = 128
PACK = 4
PASSES = K // (P * PACK)
TILES = S // P
SCALE_ROWS = 16
ES_FIRST = 48
INV_GAIN = 1.0 / 0.3
VECTOR_SHARE = (16, 84)
VECTOR_CLEARS = 1536
GPSIMD_PART = 384
TINY = 2.0 ** -120
X_PIECES = ((0, 128), (128, 256), (256, 512))


def tile_picked_ytani_sim_p_kernel(
    tc, x_words, x_scales, w1, e_words, e_scales, qn, own, offs, refs, out
):
    nc = tc.nc
    with ExitStack() as ctx:
        keep = ctx.enter_context(tc.tile_pool(name="keep", bufs=1))
        shared = ctx.enter_context(tc.tile_pool(name="shared", bufs=1))
        psum = ctx.enter_context(tc.psum_pool(name="psum", bufs=1))

        def sbuf(name, shape, dtype, tag=None, align=64):
            return keep.tile(shape, dtype, name=name, tag=tag or name, align_bytes=align)

        def placed(name, shape, dtype, offset, align=64):
            return shared.tile(shape, dtype, name=name, offset=offset, align_bytes=align)

        def bank(number, shape):
            return psum.tile(shape, F32, name="bank%d" % number)

        offs_sb = keep.tile([P, S // 16], U16, name="offs_sb")
        refs_sb = keep.tile([P, V // 16], U16, name="refs_sb")
        xs_win = sbuf("xs_win", [P, T], U8)
        es_win = sbuf("es_win", [P, W], U8)
        qn_win = sbuf("qn_win", [P, W], F32)
        own_rows = sbuf("own_rows", [P, P], F32)
        ident = sbuf("ident", [P, P], F32)
        warm = sbuf("warm", [P, 2], F32)

        nc.gpsimd.memset(xs_win[:].bitcast(I32), 0)
        nc.gpsimd.memset(qn_win[0 : P - 1, VECTOR_CLEARS:W].bitcast(I32), 0)
        nc.gpsimd.memset(es_win[0:ES_FIRST, :].bitcast(I32), 0)
        nc.gpsimd.memset(es_win[ES_FIRST + SCALE_ROWS : P, :].bitcast(I32), 0)
        nc.vector.memset(warm[:, 0:1], 1.0)
        nc.vector.memset(qn_win[0 : P - 1, 0:VECTOR_CLEARS].bitcast(I32), 0)
        nc.gpsimd.memset(own_rows[0 : P - TILES, :], 0.0)
        make_identity(nc, ident[:])
        es = sbuf("es", [P, V], U8)
        nc.gpsimd.memset(es[:].bitcast(I32), 0)
        nc.scalar.activation(warm[:, 1:2], warm[:, 0:1], ACT.Abs_reciprocal_sqrt)

        w_raw = [placed("w_raw0", [P, PACK, H], F32, 0, 256), placed("w_raw1", [P, PACK, H], F32, 8192, 256)]
        xw_win = [sbuf("xw_win%d" % o, [P, T], I32, align=256) for o in range(PASSES)]
        ew_win = sbuf("ew_win", [P, W], I32, align=256)

        def load_w(o):
            rows = w1[o * P * PACK : (o + 1) * P * PACK, :]
            nc.sync.dma_start(w_raw[o][:], rows.rearrange("(p j) c -> p j c", j=PACK))

        def load_x(o):
            nc.sync.dma_start(
                xw_win[o][:], x_words[o].rearrange("p n t -> p (n t)").bitcast(I32)
            )

        nc.sync.dma_start(qn_win[P - 1 : P, :], qn[0:1, :])
        nc.sync.dma_start(es_win[ES_FIRST : ES_FIRST + SCALE_ROWS, :].bitcast(I32), e_scales[0].bitcast(I32))
        nc.sync.dma_start(refs_sb[:], refs)
        nc.sync.dma_start(offs_sb[:], offs)
        load_w(0)
        for q in range(4):
            nc.sync.dma_start(
                xs_win[32 * q : 32 * q + 4 * PASSES, :].bitcast(I32),
                x_scales[:, 4 * q : 4 * q + 4, :].bitcast(I32),
            )
        load_x(0)
        nc.sync.dma_start(own_rows[P - TILES : P, :], own.rearrange("(j p) o -> j (p o)", p=P))
        load_w(1)
        load_x(1)

        q_row = sbuf("q_row", [P, V], F32)
        nc.vector.tensor_copy(q_row[:], qn_win[:].indirect(refs_sb[:]))
        es_picked = placed("es_picked", [P, V], U8, 16384 + 1792)
        nc.vector.tensor_copy(es_picked[:], es_win[:].indirect(refs_sb[:]))
        for q in range(4):
            if q == 3:
                nc.sync.dma_start(ew_win[:], e_words[0].rearrange("p n t -> p (n t)").bitcast(I32))
            nc.sync.dma_start(
                es[32 * q : 32 * q + 4, :].bitcast(I32),
                es_picked[ES_FIRST + 4 * q : ES_FIRST + 4 * q + 4, :].bitcast(I32),
            )

        xs = sbuf("xs", [P, S], U8)
        nc.vector.tensor_copy(xs[:], xs_win[:].indirect(offs_sb[:]))

        xw = [sbuf("xw%d" % o, [P, S], U32) for o in range(PASSES)]

        def gather_x(o, lo, hi):
            nc.vector.tensor_copy(
                xw[o][:, lo:hi],
                xw_win[o][:].bitcast(U32).indirect(offs_sb[:, lo // 16 : hi // 16]),
            )

        w_codes, w_scales = [], []

        def quantise_w(o):
            grouped = sbuf("w_grouped%d" % o, [P, PACK * H], BF16, tag="q_row" if o == 0 else None)
            src = w_raw[o][:].rearrange("p j (m t) -> p m j t", t=PACK)
            dst = grouped[:].rearrange("p (t m j) -> p m j t", t=PACK, j=PACK)
            cut = P - VECTOR_SHARE[o]
            nc.scalar.copy(dst[:, 0:cut], src[:, 0:cut])
            if cut < P:
                nc.vector.tensor_copy(dst[:, cut:P], src[:, cut:P])
            codes = sbuf("w_codes%d" % o, [P, H], U32, tag="own_rows" if o == 0 else None)
            scales = sbuf("w_scales%d" % o, [P, H], U8)
            nc.vector.quantize_mx(codes[:].bitcast(FP8X4), scales[:], grouped[:])
            w_codes.append(codes)
            w_scales.append(scales)

        turned = bank(4, [P, TILES, P])
        for b in range(V // P):
            nc.tensor.transpose(turned[:, b, :], q_row[:, b * P : (b + 1) * P], ident[:])
        q_cols = sbuf("q_cols", [P, V // P], F32)
        nc.scalar.activation(q_cols[:], turned[:, :, P - 1], ACT.Copy, scale=INV_GAIN)
        own_turned = bank(5, [P, P])
        nc.tensor.transpose(own_turned[:], own_rows[:], ident[:])
        gather_x(0, 0, S)
        quantise_w(0)

        own_cols = placed("own_cols", [P, TILES], F32, 4096)
        nc.scalar.activation(own_cols[:], own_turned[:, P - TILES : P], ACT.Copy, scale=INV_GAIN)
        spread = bank(6, [P, V])
        for b in range(V // P):
            nc.tensor.transpose(
                spread[:, b * P : (b + 1) * P], q_cols[:, b : b + 1].to_broadcast([P, P]), ident[:]
            )
        norms = {}

        def add_norms(j, offset, lo=0, hi=V):
            norms[j, lo] = placed("norms%d_%d" % (j, lo), [P, hi - lo], F32, offset + 4 * lo)
            nc.scalar.activation(norms[j, lo][:], spread[:, lo:hi], ACT.Identity, bias=own_cols[:, j : j + 1])

        add_norms(0, 0, 0, V // 2)
        add_norms(0, 0, V // 2, V)

        h_accs = [bank(j, [P, PACK, P]) for j in range(TILES)]

        def hidden_pass(j, o):
            cols = slice(j * P, (j + 1) * P)
            for t in range(PACK):
                chans = slice(t * P, (t + 1) * P)
                nc.tensor.matmul_mx(
                    h_accs[j][:, t, :],
                    lhsT=w_codes[o][:, chans].bitcast(FP8X4),
                    lhsT_scale=w_scales[o][:, chans],
                    rhs=xw[o][:, cols].bitcast(FP8X4),
                    rhs_scale=xs[4 * o : P, cols],
                    start=(o == 0 and t == 0),
                    stop=(o == PASSES - 1 and t == PACK - 1),
                )

        for j in range(TILES):
            hidden_pass(j, 0)
        quantise_w(1)
        for j in range(1, TILES):
            add_norms(j, 8192 + 2048 * j)
        for lo, hi in X_PIECES:
            gather_x(1, lo, hi)

        ew = [sbuf("ew0", [P, V // 2], U32), placed("ew1", [P, V // 2], U32, 16384 + 2048)]

        def gather_e(half):
            offsets = refs_sb[:, half * V // 32 : (half + 1) * V // 32]
            nc.vector.tensor_copy(ew[half][:], ew_win[:].bitcast(U32).indirect(offsets))

        h_words = placed("h_words", [P, S], U32, 16384)
        h_codes = [h_words[:, j * P : (j + 1) * P] for j in range(TILES)]
        h_scales_early = sbuf("h_scales_early", [P, S - P], U8)
        h_scales_last = placed("h_scales_last", [P, P], U8, 0)
        h_scales = [h_scales_early[:, j * P : (j + 1) * P] for j in range(TILES - 1)]
        h_scales.append(h_scales_last[:])
        h_grouped = {}

        def hidden(j):
            hidden_pass(j, 1)
            h_acc = h_accs[j]
            grouped = sbuf("h_grouped%d" % j, [P, P, PACK], BF16)
            nc.scalar.copy(grouped[:], h_acc[:].rearrange("p t n -> p n t"))
            h_grouped[j] = grouped

        def quantise_h(j):
            nc.vector.quantize_mx(
                h_codes[j].bitcast(FP8X4),
                h_scales[j],
                h_grouped[j][:].rearrange("p n t -> p (n t)"),
            )

        def product(j, half, acc):
            nc.tensor.matmul_mx(
                acc,
                lhsT=h_codes[j].bitcast(FP8X4),
                lhsT_scale=h_scales[j],
                rhs=ew[half][:].bitcast(FP8X4),
                rhs_scale=es[:, half * V // 2 : (half + 1) * V // 2],
                start=True,
                stop=True,
            )

        def products(j):
            if j == 0:
                halves = [bank(TILES, [P, V // 2]), bank(0, [P, V // 2])]
                parts = [(half * V // 2, (half + 1) * V // 2, halves[half][:]) for half in range(2)]
                for half in range(2):
                    product(j, half, halves[half][:])
                return parts
            acc = bank(TILES + j, [P, V])
            for half in range(2):
                product(j, half, acc[:, half * V // 2 : (half + 1) * V // 2])
            return [(0, V, acc[:])]

        accs, dens, signs, invs, signeds, roots, units = {}, {}, {}, {}, {}, {}, {}

        def denominator(j):
            accs[j] = products(j)
            dens[j] = sbuf("den%d" % j, [P, V], F32)
            for lo, hi, acc in accs[j]:
                nc.vector.tensor_tensor(dens[j][:, lo:hi], norms[j, lo][:], acc, ALU.subtract)

        def sign(j, width=V):
            signs[j] = sbuf("sign%d" % j, [P, V], F32)
            for lo in range(0, V, width):
                part = slice(lo, lo + width)
                nc.gpsimd.tensor_scalar(signs[j][:, part], dens[j][:, part], TINY, -TINY, ALU.min, ALU.max)
            units[j] = 1.0 / TINY

        def sign_on_scalar(j):
            signs[j] = sbuf("sign%d" % j, [P, V], F32)
            nc.scalar.activation(signs[j][:], dens[j][:], ACT.Sign)
            units[j] = 1.0

        def sign_shared(j):
            signs[j] = sbuf("sign%d" % j, [P, V], F32)
            acc = accs[j][0][2]
            nc.vector.tensor_tensor(signs[j][:, 0 : V // 2], norms[j, 0][:, 0 : V // 2], acc[:, 0 : V // 2], ALU.is_gt)
            nc.scalar.activation(signs[j][:, V // 2 : V], dens[j][:, V // 2 : V], ACT.Sign)
            units[j] = None

        def root(j, width=V):
            roots[j] = sbuf("root%d" % j, [P, V], F32)
            for lo in range(0, V, width):
                part = slice(lo, lo + width)
                scale = 0.5 if units[j] is None and lo == 0 else 1.0
                nc.scalar.activation(roots[j][:, part], dens[j][:, part], ACT.Abs_reciprocal_sqrt, scale=scale)

        def square(j, lo, hi):
            if j not in invs:
                invs[j] = sbuf("inv%d" % j, [P, V], F32)
            nc.scalar.activation(invs[j][:, lo:hi], roots[j][:, lo:hi], ACT.Square)

        def inverse(j):
            root(j, V // 2)
            square(j, 0, V // 2)
            square(j, V // 2, V)

        def numerator(j):
            signeds[j] = sbuf("signed%d" % j, [P, V], F32)
            if units[j]:
                parts = [(lo, hi, acc, units[j], ALU.mult) for lo, hi, acc in accs[j]]
            else:
                acc = accs[j][0][2]
                parts = [
                    (0, V // 2, acc[:, 0 : V // 2], 0.5, ALU.subtract),
                    (V // 2, V, acc[:, V // 2 : V], 1.0, ALU.mult),
                ]
            for lo, hi, acc, unit, op in parts:
                nc.vector.scalar_tensor_tensor(signeds[j][:, lo:hi], signs[j][:, lo:hi], unit, acc, op, ALU.mult)

        results = {}

        def finish(j, engine, lo, hi):
            if j not in results:
                results[j] = sbuf("result%d" % j, [P, V], F32, align=256)
            part = slice(lo, hi)
            engine.tensor_tensor(results[j][:, part], signeds[j][:, part], invs[j][:, part], ALU.mult)

        def store(j, lo, hi):
            nc.sync.dma_start(out[j * P : (j + 1) * P, lo:hi], results[j][:, lo:hi])

        for j in range(TILES):
            hidden(j)
        gather_e(0)
        quantise_h(0)
        gather_e(1)
        for j in range(1, TILES - 1):
            quantise_h(j)
        denominator(0)
        quantise_h(TILES - 1)
        sign(0)
        inverse(0)
        denominator(1)
        sign(1)
        inverse(1)
        denominator(2)
        sign_on_scalar(2)
        root(2)
        numerator(0)
        finish(0, nc.gpsimd, 0, V)
        store(0, 0, V)
        denominator(3)
        numerator(1)
        finish(1, nc.gpsimd, 0, GPSIMD_PART)
        store(1, 0, GPSIMD_PART)
        sign_shared(3)
        square(2, 0, V)
        root(3, V // 2)
        numerator(2)
        numerator(3)
        finish(1, nc.vector, GPSIMD_PART, V)
        store(1, GPSIMD_PART, V)
        finish(2, nc.vector, 0, V)
        store(2, 0, V)
        for lo in range(0, V, V // 2):
            square(3, lo, lo + V // 2)
            finish(3, nc.vector, lo, lo + V // 2)
            store(3, lo, lo + V // 2)
